import numpy as np
import ml_dtypes


def mxq(x, axis, fmt="e4m3"):
    dtype, down = {"e4m3": (ml_dtypes.float8_e4m3fn, 7), "e5m2": (ml_dtypes.float8_e5m2, 14)}[fmt]
    v = np.moveaxis(np.asarray(x, np.float32).astype(ml_dtypes.bfloat16).astype(np.float64), axis, -1)
    blocks = v.reshape(v.shape[:-1] + (-1, 32))
    amax = np.abs(blocks).max(-1, keepdims=True)
    byte = np.maximum(np.where(amax > 0, np.frexp(amax)[1] - 1 + 127, 0) - down, 1)
    scale = np.exp2(byte - 127.0)
    codes = (blocks / scale).astype(np.float32).astype(dtype).astype(np.float64)
    return np.moveaxis((codes * scale).reshape(v.shape), -1, axis)


WIDE = False


def mx_kscale(k):
    if not WIDE:
        return np.ones(k)
    levels = np.array([10, -10, 5, -5, 0])
    if k % 512:
        return np.exp2(np.random.permutation(np.resize(levels, k // 32))).repeat(32)
    a = np.empty((k // 512, 16))
    for p in range(k // 512):
        a[p, :8] = np.random.permutation(np.resize(levels, 8))
        for g in range(8):
            far = levels[np.abs(levels - a[p, g]) >= 10]
            a[p, g + 8] = far[np.random.randint(len(far))]
    return np.exp2(a.ravel()).repeat(32)


def f64(x):
    return np.asarray(x).astype(np.float64)


def striped(idx):
    return np.tile(np.asarray(idx).reshape(-1, 16).T, (8, 1)).astype(np.uint16)


def unstriped(offs):
    return offs[:16].T.reshape(-1).astype(np.int64)


B, N, T, D, NQ = 1, 512, 2048, 512, 256


def setup_inputs():
    n = np.random.standard_normal
    idx = np.random.permutation(T)[:B * N]
    idx2 = np.random.permutation(1024)[:B * N]
    s = mx_kscale(D)[:, None]
    return {
        "qT": (n((B, D, NQ)) * s * (1.00 / np.sqrt(D))).astype(np.float32),
        "kT": (np.clip(np.round(n((D, T)) * 16), -64, 64) / 16 / s).astype(np.float32),
        "rT": (np.clip(np.round(n((D, 1024)) * 16), -64, 64) / 16 / s).astype(np.float32),
        "qn": (np.random.uniform(1.0, 4.0, (B, NQ, 1))).astype(np.float32),
        "offs": striped(idx),
        "offs2": striped(idx2),
    }


def reference(qT, kT, rT, qn, offs, offs2):
    idx = unstriped(offs)
    idx2 = unstriped(offs2)
    pick = lambda x, which: x[:, which].reshape(x.shape[0], B, -1).transpose(1, 0, 2)
    kg = pick(f64(kT), idx)
    rg = pick(f64(rT), idx2)
    ug = mxq(kg + rg, 1, "e4m3")
    qq = mxq(f64(qT), 1, "e4m3")
    a = qq.transpose(0, 2, 1) @ ug
    y = a - 0.5 * f64(qn)
    return y

@@ -1,0 +1,137 @@
+from contextlib import ExitStack
+
+import concourse.mybir as mybir
+
+N, T, R, D, NQ = 512, 2048, 1024, 512, 256
+FLOPS = 2 * D * NQ * N
+
+F32 = mybir.dt.float32
+BF16 = mybir.dt.bfloat16
+U32 = mybir.dt.uint32
+U16 = mybir.dt.uint16
+U8 = mybir.dt.uint8
+FP8X4 = mybir.dt.float8_e4m3fn_x4
+ADD = mybir.AluOpType.add
+COPY = mybir.ActivationFunctionType.Copy
+IDENTITY = mybir.ActivationFunctionType.Identity
+
+P = 128
+PACK = 4
+HALF = N // 2
+QT = NQ // P
+
+
+def tile_attend_pre_transe_f_topk_kernel(tc, qT, kT, rT, qn, offs, offs2, out):
+    nc = tc.nc
+    with ExitStack() as ctx:
+        keep = ctx.enter_context(tc.tile_pool(name="keep", bufs=1))
+        psum = ctx.enter_context(tc.psum_pool(name="psum", bufs=1))
+
+        k_list = keep.tile([P, N // 16], U16, name="k_list")
+        r_list = keep.tile([P, N // 16], U16, name="r_list")
+        k_rows = kT.rearrange("(p t) n -> p t n", t=PACK)
+        r_rows = rT.rearrange("(p t) n -> p t n", t=PACK)
+        k_tab = [keep.tile([P, T], F32, name="k_tab%d" % t) for t in range(PACK)]
+        r_tab = keep.tile([P, PACK, R], F32, name="r_tab")
+        q_raw = keep.tile([P, PACK, NQ], F32, name="q_raw")
+        qn_raw = keep.tile([P, QT], F32, name="qn_raw")
+
+        nc.sync.dma_start(out=r_tab[:, 0, :], in_=r_rows[:, 0, :])
+        nc.sync.dma_start(r_list[:], offs2)
+        nc.sync.dma_start(k_list[:], offs)
+        nc.sync.dma_start(out=qn_raw[:], in_=qn[0].rearrange("(p c) o -> p (c o)", c=QT))
+        nc.sync.dma_start(out=r_tab[:, 1:3, :], in_=r_rows[:, 1:3, :])
+        nc.sync.dma_start(out=k_tab[0][:], in_=k_rows[:, 0, :])
+        nc.sync.dma_start(out=r_tab[:, 3, :], in_=r_rows[:, 3, :])
+        for t in range(1, PACK):
+            nc.sync.dma_start(out=k_tab[t][:], in_=k_rows[:, t, :])
+        nc.sync.dma_start(out=q_raw[:], in_=qT[0].rearrange("(p t) q -> p t q", t=PACK))
+
+        bias = keep.tile([P, QT], F32, name="bias")
+        nc.scalar.activation(out=bias[:], in_=qn_raw[:], func=COPY, scale=-0.5)
+
+        k_got = keep.tile([P, PACK, N], F32, name="k_got")
+        r_got = keep.tile([P, PACK, N], F32, name="r_got")
+        u_rows = keep.tile([P, PACK, N], BF16, name="u_rows")
+        u_words = keep.tile([P, N, PACK], BF16, name="u_words", align_bytes=64)
+        u_codes = keep.tile([P, N], U32, name="u_codes", align_bytes=64)
+        u_scales = keep.tile([P, N], U8, name="u_scales", align_bytes=64)
+        q_words = keep.tile([P, QT, P, PACK], BF16, name="q_words", align_bytes=64)
+        q_codes = keep.tile([P, QT, P], U32, name="q_codes", align_bytes=64)
+        q_scales = keep.tile([P, QT, P], U8, name="q_scales", align_bytes=64)
+
+        def gather_r(t):
+            nc.vector.tensor_copy(out=r_got[:, t, :], in_=r_tab[:, t, :].indirect(r_list[:]))
+
+        def gather_k(t, lo, hi):
+            nc.vector.tensor_copy(out=k_got[:, t, lo:hi], in_=k_tab[t][:].indirect(k_list[:, lo // 16 : hi // 16]))
+
+        def add(t, lo, hi):
+            nc.vector.tensor_tensor(out=u_rows[:, t, lo:hi], in0=k_got[:, t, lo:hi], in1=r_got[:, t, lo:hi], op=ADD)
+
+        gather_r(0)
+        gather_r(1)
+        gather_r(2)
+        gather_k(0, 0, N)
+        gather_r(3)
+        add(0, 0, N)
+        gather_k(1, 0, N)
+        add(1, 0, N)
+        nc.scalar.activation(out=u_words[:, :, 0:2], in_=u_rows[:, 0:2, :].rearrange("p t n -> p n t"), func=COPY)
+        gather_k(2, 0, N)
+        add(2, 0, N)
+
+        q_by_tile = q_raw[:].rearrange("p t (j i c) -> p c j t i", i=2, c=QT)
+        for c in range(QT):
+            nc.scalar.activation(
+                out=q_words[:, c, :, :].rearrange("p (j i) t -> p j t i", i=2), in_=q_by_tile[:, c, :, :, :], func=COPY
+            )
+
+        halves = [(0, HALF), (HALF, N)]
+        for lo, hi in halves:
+            gather_k(3, lo, hi)
+        for lo, hi in halves:
+            add(3, lo, hi)
+
+        res = keep.tile([P, QT, N], F32, name="res")
+        out_rows = out[0].rearrange("(p c) n -> p c n", c=QT)
+
+        def product(h, c):
+            lo, hi = halves[h]
+            acc = psum.tile([P, HALF], F32, name="acc%d%d" % (h, c))
+            nc.tensor.matmul_mx(
+                out=acc[:],
+                lhsT=q_codes[:, c, :].bitcast(FP8X4),
+                lhsT_scale=q_scales[:, c, :],
+                rhs=u_codes[:, lo:hi].bitcast(FP8X4),
+                rhs_scale=u_scales[:, lo:hi],
+                start=True,
+                stop=True,
+            )
+            if (h, c) == (1, 0):
+                nc.vector.tensor_scalar(out=res[:, c, lo:hi], in0=acc[:], scalar1=bias[:, c : c + 1], scalar2=None, op0=ADD)
+                nc.sync.dma_start(out=out_rows[:, c, lo:hi], in_=res[:, c, lo:hi])
+            else:
+                nc.scalar.activation(out=res[:, c, lo:hi], in_=acc[:], func=IDENTITY, bias=bias[:, c : c + 1])
+                eng = nc.scalar if h == 1 else nc.sync
+                eng.dma_start(out=out_rows[:, c, lo:hi], in_=res[:, c, lo:hi])
+
+        for h in range(2):
+            lo, hi = halves[h]
+            nc.vector.tensor_copy(out=u_words[:, lo:hi, 2:4], in_=u_rows[:, 2:4, lo:hi].rearrange("p t n -> p n t"))
+            nc.vector.quantize_mx(
+                out=q_codes[:, h, :].bitcast(FP8X4),
+                scales=q_scales[:, h, :],
+                in_=q_words[:, h, :, :].rearrange("p m t -> p (m t)"),
+            )
+            nc.vector.quantize_mx(
+                out=u_codes[:, lo:hi].bitcast(FP8X4),
+                scales=u_scales[:, lo:hi],
+                in_=u_words[:, lo:hi, :].rearrange("p n t -> p (n t)"),
+            )
+            if h == 0:
+                product(0, 0)
+            else:
+                product(0, 1)
+                product(1, 0)
+                product(1, 1)

@@ -19,6 +19,7 @@ P = 128
 PACK = 4
 HALF = N // 2
 QT = NQ // P
+CHUNKS = [(0, 256), (256, 512)]
 
 
 def tile_attend_pre_transe_f_topk_kernel(tc, qT, kT, rT, qn, offs, offs2, out):
@@ -50,12 +51,12 @@ def tile_attend_pre_transe_f_topk_kernel(tc, qT, kT, rT, qn, offs, offs2, out):
         bias = keep.tile([P, QT], F32, name="bias")
         nc.scalar.activation(out=bias[:], in_=qn_raw[:], func=COPY, scale=-0.5)
 
-        k_got = keep.tile([P, PACK, N], F32, name="k_got")
+        k_got = keep.tile([P, PACK - 1, N], F32, name="k_got")
         r_got = keep.tile([P, PACK, N], F32, name="r_got")
         u_rows = keep.tile([P, PACK, N], BF16, name="u_rows")
-        u_words = keep.tile([P, N, PACK], BF16, name="u_words", align_bytes=64)
-        u_codes = keep.tile([P, N], U32, name="u_codes", align_bytes=64)
-        u_scales = keep.tile([P, N], U8, name="u_scales", align_bytes=64)
+        u_words = [keep.tile([P, hi - lo, PACK], BF16, name="u_words%d" % lo, align_bytes=64) for lo, hi in CHUNKS]
+        u_codes = [keep.tile([P, HALF], U32, name="u_codes0", align_bytes=64)]
+        u_scales = [keep.tile([P, hi - lo], U8, name="u_scales%d" % lo, align_bytes=64) for lo, hi in CHUNKS]
         q_words = keep.tile([P, QT, P, PACK], BF16, name="q_words", align_bytes=64)
         q_codes = keep.tile([P, QT, P], U32, name="q_codes", align_bytes=64)
         q_scales = keep.tile([P, QT, P], U8, name="q_scales", align_bytes=64)
@@ -63,75 +64,86 @@ def tile_attend_pre_transe_f_topk_kernel(tc, qT, kT, rT, qn, offs, offs2, out):
         def gather_r(t):
             nc.vector.tensor_copy(out=r_got[:, t, :], in_=r_tab[:, t, :].indirect(r_list[:]))
 
-        def gather_k(t, lo, hi):
-            nc.vector.tensor_copy(out=k_got[:, t, lo:hi], in_=k_tab[t][:].indirect(k_list[:, lo // 16 : hi // 16]))
+        def gather_k(t):
+            nc.vector.tensor_copy(out=k_got[:, t, :], in_=k_tab[t][:].indirect(k_list[:]))
 
-        def add(t, lo, hi):
-            nc.vector.tensor_tensor(out=u_rows[:, t, lo:hi], in0=k_got[:, t, lo:hi], in1=r_got[:, t, lo:hi], op=ADD)
+        def add(t):
+            nc.vector.tensor_tensor(out=u_rows[:, t, :], in0=k_got[:, t, :], in1=r_got[:, t, :], op=ADD)
+
+        def pack(eng, h, t):
+            lo, hi = CHUNKS[h]
+            src = u_rows[:, t : t + 2, lo:hi].rearrange("p t n -> p n t")
+            if eng == "v":
+                nc.vector.tensor_copy(out=u_words[h][:, :, t : t + 2], in_=src)
+            else:
+                nc.scalar.activation(out=u_words[h][:, :, t : t + 2], in_=src, func=COPY)
 
         gather_r(0)
         gather_r(1)
         gather_r(2)
-        gather_k(0, 0, N)
+        gather_k(0)
         gather_r(3)
-        add(0, 0, N)
-        gather_k(1, 0, N)
-        add(1, 0, N)
-        nc.scalar.activation(out=u_words[:, :, 0:2], in_=u_rows[:, 0:2, :].rearrange("p t n -> p n t"), func=COPY)
-        gather_k(2, 0, N)
-        add(2, 0, N)
+        add(0)
+        gather_k(1)
+        add(1)
+        for h in range(2):
+            pack("s", h, 0)
+        gather_k(2)
+        add(2)
 
-        q_by_tile = q_raw[:].rearrange("p t (j i c) -> p c j t i", i=2, c=QT)
-        for c in range(QT):
-            nc.scalar.activation(
-                out=q_words[:, c, :, :].rearrange("p (j i) t -> p j t i", i=2), in_=q_by_tile[:, c, :, :, :], func=COPY
-            )
+        nc.scalar.activation(
+            out=q_words[:].rearrange("p c m t -> p m t c"),
+            in_=q_raw[:].rearrange("p t (m c) -> p m t c", c=QT),
+            func=COPY,
+        )
 
-        halves = [(0, HALF), (HALF, N)]
-        for lo, hi in halves:
-            gather_k(3, lo, hi)
-        for lo, hi in halves:
-            add(3, lo, hi)
+        k_last = [keep.tile([P, HALF], F32, name="k_last%d" % h, align_bytes=64) for h in range(2)]
+        for h in range(2):
+            nc.vector.tensor_copy(out=k_last[h][:], in_=k_tab[3][:].indirect(k_list[:, 16 * h : 16 * h + 16]))
+        for h in range(2):
+            cols = slice(h * HALF, (h + 1) * HALF)
+            nc.vector.tensor_tensor(out=u_rows[:, 3, cols], in0=k_last[h][:], in1=r_got[:, 3, cols], op=ADD)
 
         res = keep.tile([P, QT, N], F32, name="res")
         out_rows = out[0].rearrange("(p c) n -> p c n", c=QT)
 
+        def quant_u(h):
+            nc.vector.quantize_mx(
+                out=u_codes[h][:].bitcast(FP8X4),
+                scales=u_scales[h][:],
+                in_=u_words[h][:].rearrange("p n t -> p (n t)"),
+            )
+
         def product(h, c):
-            lo, hi = halves[h]
-            acc = psum.tile([P, HALF], F32, name="acc%d%d" % (h, c))
+            lo, hi = CHUNKS[h]
+            acc = psum.tile([P, hi - lo], F32, name="acc%d%d" % (h, c))
             nc.tensor.matmul_mx(
                 out=acc[:],
                 lhsT=q_codes[:, c, :].bitcast(FP8X4),
                 lhsT_scale=q_scales[:, c, :],
-                rhs=u_codes[:, lo:hi].bitcast(FP8X4),
-                rhs_scale=u_scales[:, lo:hi],
+                rhs=u_codes[h][:].bitcast(FP8X4),
+                rhs_scale=u_scales[h][:],
                 start=True,
                 stop=True,
             )
-            if (h, c) == (1, 0):
+            if h > 0 and c == 0:
                 nc.vector.tensor_scalar(out=res[:, c, lo:hi], in0=acc[:], scalar1=bias[:, c : c + 1], scalar2=None, op0=ADD)
-                nc.sync.dma_start(out=out_rows[:, c, lo:hi], in_=res[:, c, lo:hi])
             else:
                 nc.scalar.activation(out=res[:, c, lo:hi], in_=acc[:], func=IDENTITY, bias=bias[:, c : c + 1])
-                eng = nc.scalar if h == 1 else nc.sync
-                eng.dma_start(out=out_rows[:, c, lo:hi], in_=res[:, c, lo:hi])
 
+        pack("v", 0, 2)
+        pack("v", 1, 2)
+        quant_u(0)
+        nc.vector.quantize_mx(
+            out=q_codes[:].rearrange("p c m -> p (c m)").bitcast(FP8X4),
+            scales=q_scales[:].rearrange("p c m -> p (c m)"),
+            in_=q_words[:].rearrange("p c m t -> p (c m t)"),
+        )
+        u_codes.append(keep.tile([P, HALF], U32, name="u_codes1", tag="q_words", align_bytes=64))
+        quant_u(1)
         for h in range(2):
-            lo, hi = halves[h]
-            nc.vector.tensor_copy(out=u_words[:, lo:hi, 2:4], in_=u_rows[:, 2:4, lo:hi].rearrange("p t n -> p n t"))
-            nc.vector.quantize_mx(
-                out=q_codes[:, h, :].bitcast(FP8X4),
-                scales=q_scales[:, h, :],
-                in_=q_words[:, h, :, :].rearrange("p m t -> p (m t)"),
-            )
-            nc.vector.quantize_mx(
-                out=u_codes[:, lo:hi].bitcast(FP8X4),
-                scales=u_scales[:, lo:hi],
-                in_=u_words[:, lo:hi, :].rearrange("p n t -> p (n t)"),
-            )
-            if h == 0:
-                product(0, 0)
-            else:
-                product(0, 1)
-                product(1, 0)
-                product(1, 1)
+            for c in range(QT):
+                product(h, c)
+                lo, hi = CHUNKS[h]
+                eng = nc.scalar if (h, c) == (1, 1) else nc.sync
+                eng.dma_start(out=out_rows[:, c, lo:hi], in_=res[:, c, lo:hi])

@@ -19,7 +19,8 @@ P = 128
 PACK = 4
 HALF = N // 2
 QT = NQ // P
-CHUNKS = [(0, 256), (256, 512)]
+W = 128
+CH = N // W
 
 
 def tile_attend_pre_transe_f_topk_kernel(tc, qT, kT, rT, qn, offs, offs2, out):
@@ -32,34 +33,34 @@ def tile_attend_pre_transe_f_topk_kernel(tc, qT, kT, rT, qn, offs, offs2, out):
         r_list = keep.tile([P, N // 16], U16, name="r_list")
         k_rows = kT.rearrange("(p t) n -> p t n", t=PACK)
         r_rows = rT.rearrange("(p t) n -> p t n", t=PACK)
+        q_rows = qT[0].rearrange("(p t) q -> p t q", t=PACK)
         k_tab = [keep.tile([P, T], F32, name="k_tab%d" % t) for t in range(PACK)]
         r_tab = keep.tile([P, PACK, R], F32, name="r_tab")
-        q_raw = keep.tile([P, PACK, NQ], F32, name="q_raw")
+        q_raw = [keep.tile([P, PACK, P], F32, name="q_raw%d" % c, align_bytes=64) for c in range(QT)]
         qn_raw = keep.tile([P, QT], F32, name="qn_raw")
 
         nc.sync.dma_start(out=r_tab[:, 0, :], in_=r_rows[:, 0, :])
         nc.sync.dma_start(r_list[:], offs2)
         nc.sync.dma_start(k_list[:], offs)
-        nc.sync.dma_start(out=qn_raw[:], in_=qn[0].rearrange("(p c) o -> p (c o)", c=QT))
         nc.sync.dma_start(out=r_tab[:, 1:3, :], in_=r_rows[:, 1:3, :])
         nc.sync.dma_start(out=k_tab[0][:], in_=k_rows[:, 0, :])
         nc.sync.dma_start(out=r_tab[:, 3, :], in_=r_rows[:, 3, :])
         for t in range(1, PACK):
             nc.sync.dma_start(out=k_tab[t][:], in_=k_rows[:, t, :])
-        nc.sync.dma_start(out=q_raw[:], in_=qT[0].rearrange("(p t) q -> p t q", t=PACK))
-
-        bias = keep.tile([P, QT], F32, name="bias")
-        nc.scalar.activation(out=bias[:], in_=qn_raw[:], func=COPY, scale=-0.5)
+        for c in range(QT):
+            nc.sync.dma_start(out=q_raw[c][:], in_=q_rows[:, :, c * P : (c + 1) * P])
+        with nc.allow_non_contiguous_dma(reason="one squared length a partition and query tile"):
+            nc.sync.dma_start(out=qn_raw[:], in_=qn[0].rearrange("(c p) o -> p (c o)", c=QT))
 
         k_got = keep.tile([P, PACK - 1, N], F32, name="k_got")
         r_got = keep.tile([P, PACK, N], F32, name="r_got")
         u_rows = keep.tile([P, PACK, N], BF16, name="u_rows")
-        u_words = [keep.tile([P, hi - lo, PACK], BF16, name="u_words%d" % lo, align_bytes=64) for lo, hi in CHUNKS]
-        u_codes = [keep.tile([P, HALF], U32, name="u_codes0", align_bytes=64)]
-        u_scales = [keep.tile([P, hi - lo], U8, name="u_scales%d" % lo, align_bytes=64) for lo, hi in CHUNKS]
-        q_words = keep.tile([P, QT, P, PACK], BF16, name="q_words", align_bytes=64)
-        q_codes = keep.tile([P, QT, P], U32, name="q_codes", align_bytes=64)
-        q_scales = keep.tile([P, QT, P], U8, name="q_scales", align_bytes=64)
+        u_words = {h: keep.tile([P, W, PACK], BF16, name="u_words%d" % h, align_bytes=64)[:] for h in (0, 3)}
+        u_scales = [keep.tile([P, W], U8, name="u_scales%d" % h, align_bytes=64) for h in range(CH)]
+        q_words = [keep.tile([P, P, PACK], BF16, name="q_words%d" % c, align_bytes=64) for c in range(QT)]
+        q_codes = [keep.tile([P, P], U32, name="q_codes%d" % c, align_bytes=64) for c in range(QT)]
+        q_scales = [keep.tile([P, P], U8, name="q_scales%d" % c, align_bytes=64) for c in range(QT)]
+        bias = keep.tile([P, QT], F32, name="bias")
 
         def gather_r(t):
             nc.vector.tensor_copy(out=r_got[:, t, :], in_=r_tab[:, t, :].indirect(r_list[:]))
@@ -71,12 +72,31 @@ def tile_attend_pre_transe_f_topk_kernel(tc, qT, kT, rT, qn, offs, offs2, out):
             nc.vector.tensor_tensor(out=u_rows[:, t, :], in0=k_got[:, t, :], in1=r_got[:, t, :], op=ADD)
 
         def pack(eng, h, t):
-            lo, hi = CHUNKS[h]
-            src = u_rows[:, t : t + 2, lo:hi].rearrange("p t n -> p n t")
+            src = u_rows[:, t : t + 2, h * W : (h + 1) * W].rearrange("p t n -> p n t")
             if eng == "v":
                 nc.vector.tensor_copy(out=u_words[h][:, :, t : t + 2], in_=src)
             else:
                 nc.scalar.activation(out=u_words[h][:, :, t : t + 2], in_=src, func=COPY)
+
+        def cast_q(c):
+            nc.scalar.activation(
+                out=q_words[c][:].rearrange("p (g i) t -> p g t i", i=4),
+                in_=q_raw[c][:].rearrange("p t (g i) -> p g t i", i=4),
+                func=COPY,
+            )
+
+        def quant_q(c):
+            nc.vector.quantize_mx(
+                out=q_codes[c][:].bitcast(FP8X4), scales=q_scales[c][:], in_=q_words[c][:].rearrange("p m t -> p (m t)")
+            )
+
+        u_codes = {}
+
+        def quant_u(h, tag):
+            u_codes[h] = keep.tile([P, W], U32, name="u_codes%d" % h, tag=tag, align_bytes=64)
+            nc.vector.quantize_mx(
+                out=u_codes[h][:].bitcast(FP8X4), scales=u_scales[h][:], in_=u_words[h].rearrange("p n t -> p (n t)")
+            )
 
         gather_r(0)
         gather_r(1)
@@ -86,16 +106,14 @@ def tile_attend_pre_transe_f_topk_kernel(tc, qT, kT, rT, qn, offs, offs2, out):
         add(0)
         gather_k(1)
         add(1)
-        for h in range(2):
+        for h in (0, 3):
             pack("s", h, 0)
         gather_k(2)
         add(2)
 
-        nc.scalar.activation(
-            out=q_words[:].rearrange("p c m t -> p m t c"),
-            in_=q_raw[:].rearrange("p t (m c) -> p m t c", c=QT),
-            func=COPY,
-        )
+        for c in range(QT):
+            cast_q(c)
+        nc.scalar.activation(out=bias[:], in_=qn_raw[:], func=COPY, scale=-0.5)
 
         k_last = [keep.tile([P, HALF], F32, name="k_last%d" % h, align_bytes=64) for h in range(2)]
         for h in range(2):
@@ -104,46 +122,50 @@ def tile_attend_pre_transe_f_topk_kernel(tc, qT, kT, rT, qn, offs, offs2, out):
             cols = slice(h * HALF, (h + 1) * HALF)
             nc.vector.tensor_tensor(out=u_rows[:, 3, cols], in0=k_last[h][:], in1=r_got[:, 3, cols], op=ADD)
 
-        res = keep.tile([P, QT, N], F32, name="res")
-        out_rows = out[0].rearrange("(p c) n -> p c n", c=QT)
+        res = {h: keep.tile([P, QT, W], F32, name="res%d" % h)[:] for h in (0, 3)}
+        out_rows = out[0].rearrange("(c p) n -> p c n", c=QT)
 
-        def quant_u(h):
-            nc.vector.quantize_mx(
-                out=u_codes[h][:].bitcast(FP8X4),
-                scales=u_scales[h][:],
-                in_=u_words[h][:].rearrange("p n t -> p (n t)"),
-            )
-
-        def product(h, c):
-            lo, hi = CHUNKS[h]
-            acc = psum.tile([P, hi - lo], F32, name="acc%d%d" % (h, c))
+        def product(h, c, eng):
+            acc = psum.tile([P, W], F32, name="acc%d%d" % (h, c))
             nc.tensor.matmul_mx(
                 out=acc[:],
-                lhsT=q_codes[:, c, :].bitcast(FP8X4),
-                lhsT_scale=q_scales[:, c, :],
+                lhsT=q_codes[c][:].bitcast(FP8X4),
+                lhsT_scale=q_scales[c][:],
                 rhs=u_codes[h][:].bitcast(FP8X4),
                 rhs_scale=u_scales[h][:],
                 start=True,
                 stop=True,
             )
-            if h > 0 and c == 0:
-                nc.vector.tensor_scalar(out=res[:, c, lo:hi], in0=acc[:], scalar1=bias[:, c : c + 1], scalar2=None, op0=ADD)
+            if eng == "v":
+                nc.vector.tensor_scalar(out=res[h][:, c, :], in0=acc[:], scalar1=bias[:, c : c + 1], scalar2=None, op0=ADD)
             else:
-                nc.scalar.activation(out=res[:, c, lo:hi], in_=acc[:], func=IDENTITY, bias=bias[:, c : c + 1])
+                nc.scalar.activation(out=res[h][:, c, :], in_=acc[:], func=IDENTITY, bias=bias[:, c : c + 1])
 
         pack("v", 0, 2)
-        pack("v", 1, 2)
-        quant_u(0)
-        nc.vector.quantize_mx(
-            out=q_codes[:].rearrange("p c m -> p (c m)").bitcast(FP8X4),
-            scales=q_scales[:].rearrange("p c m -> p (c m)"),
-            in_=q_words[:].rearrange("p c m t -> p (c m t)"),
-        )
-        u_codes.append(keep.tile([P, HALF], U32, name="u_codes1", tag="q_words", align_bytes=64))
-        quant_u(1)
-        for h in range(2):
-            for c in range(QT):
-                product(h, c)
-                lo, hi = CHUNKS[h]
-                eng = nc.scalar if (h, c) == (1, 1) else nc.sync
-                eng.dma_start(out=out_rows[:, c, lo:hi], in_=res[:, c, lo:hi])
+        pack("v", 3, 2)
+        mid_words = keep.tile([P, 2, W, PACK], BF16, name="mid_words", tag="q_raw1", align_bytes=64)
+        for h in (1, 2):
+            u_words[h] = mid_words[:, h - 1, :, :]
+            nc.scalar.activation(
+                out=u_words[h].rearrange("p (g i) t -> p g t i", i=4),
+                in_=u_rows[:, :, h * W : (h + 1) * W].rearrange("p t (g i) -> p g t i", i=4),
+                func=COPY,
+            )
+        quant_q(0)
+        quant_u(0, "q_words0")
+        quant_q(1)
+        quant_u(3, "u_words0")
+        quant_u(1, "q_words1")
+        quant_u(2, "u_words3")
+        mid_res = keep.tile([P, 2, QT, W], F32, name="mid_res", tag="q_raw1", align_bytes=64)
+        for h in (1, 2):
+            res[h] = mid_res[:, h - 1, :, :]
+        for h in (0, 3, 1, 2):
+            cols = slice(h * W, (h + 1) * W)
+            product(h, 0, "v" if h == 1 else "s")
+            product(h, 1, "s" if h in (0, 3) else "v")
+            if h != 2:
+                nc.sync.dma_start(out=out_rows[:, :, cols], in_=res[h])
+            else:
+                nc.scalar.dma_start(out=out_rows[:, 0, cols], in_=res[h][:, 0, :])
+                nc.sync.dma_start(out=out_rows[:, 1, cols], in_=res[h][:, 1, :])

@@ -1,6 +1,7 @@
 from contextlib import ExitStack
 
 import concourse.mybir as mybir
+from concourse.masks import make_identity
 
 N, T, R, D, NQ = 512, 2048, 1024, 512, 256
 FLOPS = 2 * D * NQ * N
@@ -37,11 +38,15 @@ def tile_attend_pre_transe_f_topk_kernel(tc, qT, kT, rT, qn, offs, offs2, out):
         k_tab = [keep.tile([P, T], F32, name="k_tab%d" % t) for t in range(PACK)]
         r_tab = keep.tile([P, PACK, R], F32, name="r_tab")
         q_raw = [keep.tile([P, PACK, P], F32, name="q_raw%d" % c, align_bytes=64) for c in range(QT)]
-        qn_raw = keep.tile([P, QT], F32, name="qn_raw")
+        qn_rows = keep.tile([P, P], F32, name="qn_rows")
+        ident = keep.tile([P, P], F32, name="ident")
+        nc.gpsimd.memset(qn_rows[:], 0.0)
+        make_identity(nc, ident[:])
 
         nc.sync.dma_start(out=r_tab[:, 0, :], in_=r_rows[:, 0, :])
         nc.sync.dma_start(r_list[:], offs2)
         nc.sync.dma_start(k_list[:], offs)
+        nc.sync.dma_start(out=qn_rows[0:QT, :], in_=qn[0].rearrange("(c p) o -> c (p o)", c=QT))
         nc.sync.dma_start(out=r_tab[:, 1:3, :], in_=r_rows[:, 1:3, :])
         nc.sync.dma_start(out=k_tab[0][:], in_=k_rows[:, 0, :])
         nc.sync.dma_start(out=r_tab[:, 3, :], in_=r_rows[:, 3, :])
@@ -49,8 +54,6 @@ def tile_attend_pre_transe_f_topk_kernel(tc, qT, kT, rT, qn, offs, offs2, out):
             nc.sync.dma_start(out=k_tab[t][:], in_=k_rows[:, t, :])
         for c in range(QT):
             nc.sync.dma_start(out=q_raw[c][:], in_=q_rows[:, :, c * P : (c + 1) * P])
-        with nc.allow_non_contiguous_dma(reason="one squared length a partition and query tile"):
-            nc.sync.dma_start(out=qn_raw[:], in_=qn[0].rearrange("(c p) o -> p (c o)", c=QT))
 
         k_got = keep.tile([P, PACK - 1, N], F32, name="k_got")
         r_got = keep.tile([P, PACK, N], F32, name="r_got")
@@ -80,8 +83,8 @@ def tile_attend_pre_transe_f_topk_kernel(tc, qT, kT, rT, qn, offs, offs2, out):
 
         def cast_q(c):
             nc.scalar.activation(
-                out=q_words[c][:].rearrange("p (g i) t -> p g t i", i=4),
-                in_=q_raw[c][:].rearrange("p t (g i) -> p g t i", i=4),
+                out=q_words[c][:],
+                in_=q_raw[c][:].rearrange("p t m -> p m t"),
                 func=COPY,
             )
 
@@ -98,6 +101,10 @@ def tile_attend_pre_transe_f_topk_kernel(tc, qT, kT, rT, qn, offs, offs2, out):
                 out=u_codes[h][:].bitcast(FP8X4), scales=u_scales[h][:], in_=u_words[h].rearrange("p n t -> p (n t)")
             )
 
+        qn_cols = psum.tile([P, P], F32, name="qn_cols", tag="acc21")
+        nc.tensor.transpose(qn_cols[:], qn_rows[:], ident[:])
+        nc.scalar.activation(out=bias[:], in_=qn_cols[:, 0:QT], func=COPY, scale=-0.5)
+
         gather_r(0)
         gather_r(1)
         gather_r(2)
@@ -113,7 +120,6 @@ def tile_attend_pre_transe_f_topk_kernel(tc, qT, kT, rT, qn, offs, offs2, out):
 
         for c in range(QT):
             cast_q(c)
-        nc.scalar.activation(out=bias[:], in_=qn_raw[:], func=COPY, scale=-0.5)
 
         k_last = [keep.tile([P, HALF], F32, name="k_last%d" % h, align_bytes=64) for h in range(2)]
         for h in range(2):
@@ -147,8 +153,8 @@ def tile_attend_pre_transe_f_topk_kernel(tc, qT, kT, rT, qn, offs, offs2, out):
         for h in (1, 2):
             u_words[h] = mid_words[:, h - 1, :, :]
             nc.scalar.activation(
-                out=u_words[h].rearrange("p (g i) t -> p g t i", i=4),
-                in_=u_rows[:, :, h * W : (h + 1) * W].rearrange("p t (g i) -> p g t i", i=4),
+                out=u_words[h],
+                in_=u_rows[:, :, h * W : (h + 1) * W].rearrange("p t n -> p n t"),
                 func=COPY,
             )
         quant_q(0)

@@ -34,31 +34,30 @@ def tile_attend_pre_transe_f_topk_kernel(tc, qT, kT, rT, qn, offs, offs2, out):
         r_list = keep.tile([P, N // 16], U16, name="r_list")
         k_rows = kT.rearrange("(p t) n -> p t n", t=PACK)
         r_rows = rT.rearrange("(p t) n -> p t n", t=PACK)
-        q_rows = qT[0].rearrange("(p t) q -> p t q", t=PACK)
         k_tab = [keep.tile([P, T], F32, name="k_tab%d" % t) for t in range(PACK)]
         r_tab = keep.tile([P, PACK, R], F32, name="r_tab")
-        q_raw = [keep.tile([P, PACK, P], F32, name="q_raw%d" % c, align_bytes=64) for c in range(QT)]
+        q_raw = keep.tile([P, PACK, NQ], F32, name="q_raw", align_bytes=64)
         qn_rows = keep.tile([P, P], F32, name="qn_rows")
         ident = keep.tile([P, P], F32, name="ident")
-        nc.gpsimd.memset(qn_rows[:], 0.0)
+        nc.vector.memset(qn_rows[:], 0.0)
         make_identity(nc, ident[:])
 
         nc.sync.dma_start(out=r_tab[:, 0, :], in_=r_rows[:, 0, :])
         nc.sync.dma_start(r_list[:], offs2)
         nc.sync.dma_start(k_list[:], offs)
-        nc.sync.dma_start(out=qn_rows[0:QT, :], in_=qn[0].rearrange("(c p) o -> c (p o)", c=QT))
         nc.sync.dma_start(out=r_tab[:, 1:3, :], in_=r_rows[:, 1:3, :])
         nc.sync.dma_start(out=k_tab[0][:], in_=k_rows[:, 0, :])
+        nc.sync.dma_start(out=qn_rows[0:QT, :], in_=qn[0].rearrange("(c p) o -> c (p o)", c=QT))
         nc.sync.dma_start(out=r_tab[:, 3, :], in_=r_rows[:, 3, :])
         for t in range(1, PACK):
             nc.sync.dma_start(out=k_tab[t][:], in_=k_rows[:, t, :])
-        for c in range(QT):
-            nc.sync.dma_start(out=q_raw[c][:], in_=q_rows[:, :, c * P : (c + 1) * P])
+        nc.sync.dma_start(out=q_raw[:], in_=qT[0].rearrange("(p t) q -> p t q", t=PACK))
 
         k_got = keep.tile([P, PACK - 1, N], F32, name="k_got")
         r_got = keep.tile([P, PACK, N], F32, name="r_got")
+        k_last = [keep.tile([P, HALF], F32, name="k_last%d" % a) for a in range(2)]
         u_rows = keep.tile([P, PACK, N], BF16, name="u_rows")
-        u_words = {h: keep.tile([P, W, PACK], BF16, name="u_words%d" % h, align_bytes=64)[:] for h in (0, 3)}
+        u_words = [keep.tile([P, W, PACK], BF16, name="u_words%d" % h, align_bytes=64) for h in range(CH)]
         u_scales = [keep.tile([P, W], U8, name="u_scales%d" % h, align_bytes=64) for h in range(CH)]
         q_words = [keep.tile([P, P, PACK], BF16, name="q_words%d" % c, align_bytes=64) for c in range(QT)]
         q_codes = [keep.tile([P, P], U32, name="q_codes%d" % c, align_bytes=64) for c in range(QT)]
@@ -74,18 +73,21 @@ def tile_attend_pre_transe_f_topk_kernel(tc, qT, kT, rT, qn, offs, offs2, out):
         def add(t):
             nc.vector.tensor_tensor(out=u_rows[:, t, :], in0=k_got[:, t, :], in1=r_got[:, t, :], op=ADD)
 
-        def pack(eng, h, t):
-            src = u_rows[:, t : t + 2, h * W : (h + 1) * W].rearrange("p t n -> p n t")
+        def pack(eng, h, lo, src):
+            planes = src.shape[1]
+            dst = u_words[h][:, :, lo : lo + planes]
             if eng == "v":
-                nc.vector.tensor_copy(out=u_words[h][:, :, t : t + 2], in_=src)
+                nc.vector.tensor_copy(out=dst, in_=src.rearrange("p t n -> p n t"))
             else:
-                nc.scalar.activation(out=u_words[h][:, :, t : t + 2], in_=src, func=COPY)
+                nc.scalar.activation(out=dst, in_=src.rearrange("p t n -> p n t"), func=COPY)
+
+        def rows(h, lo, hi):
+            return u_rows[:, lo:hi, h * W : (h + 1) * W]
 
         def cast_q(c):
-            nc.scalar.activation(
-                out=q_words[c][:],
-                in_=q_raw[c][:].rearrange("p t m -> p m t"),
-                func=COPY,
+            nc.vector.tensor_copy(
+                out=q_words[c][:].rearrange("p (g i) t -> p g t i", i=2),
+                in_=q_raw[:, :, c * P : (c + 1) * P].rearrange("p t (g i) -> p g t i", i=2),
             )
 
         def quant_q(c):
@@ -95,13 +97,12 @@ def tile_attend_pre_transe_f_topk_kernel(tc, qT, kT, rT, qn, offs, offs2, out):
 
         u_codes = {}
 
-        def quant_u(h, tag):
-            u_codes[h] = keep.tile([P, W], U32, name="u_codes%d" % h, tag=tag, align_bytes=64)
+        def quant_u(h):
             nc.vector.quantize_mx(
-                out=u_codes[h][:].bitcast(FP8X4), scales=u_scales[h][:], in_=u_words[h].rearrange("p n t -> p (n t)")
+                out=u_codes[h].bitcast(FP8X4), scales=u_scales[h][:], in_=u_words[h][:].rearrange("p n t -> p (n t)")
             )
 
-        qn_cols = psum.tile([P, P], F32, name="qn_cols", tag="acc21")
+        qn_cols = psum.tile([P, P], F32, name="qn_cols", tag="turn")
         nc.tensor.transpose(qn_cols[:], qn_rows[:], ident[:])
         nc.scalar.activation(out=bias[:], in_=qn_cols[:, 0:QT], func=COPY, scale=-0.5)
 
@@ -113,65 +114,64 @@ def tile_attend_pre_transe_f_topk_kernel(tc, qT, kT, rT, qn, offs, offs2, out):
         add(0)
         gather_k(1)
         add(1)
-        for h in (0, 3):
-            pack("s", h, 0)
+        for h in range(CH):
+            pack("s", h, 0, rows(h, 0, 2))
         gather_k(2)
         add(2)
 
-        for c in range(QT):
-            cast_q(c)
+        for a in range(2):
+            nc.vector.tensor_copy(out=k_last[a][:], in_=k_tab[3][:].indirect(k_list[:, 16 * a : 16 * a + 16]))
+        for h in range(CH):
+            cols = slice(h * W, (h + 1) * W)
+            got = k_last[h // 2][:, (h % 2) * W : (h % 2 + 1) * W]
+            nc.vector.tensor_tensor(out=u_rows[:, 3, cols], in0=got, in1=r_got[:, 3, cols], op=ADD)
+            pack("s", h, 2, rows(h, 2, 4))
 
-        k_last = [keep.tile([P, HALF], F32, name="k_last%d" % h, align_bytes=64) for h in range(2)]
-        for h in range(2):
-            nc.vector.tensor_copy(out=k_last[h][:], in_=k_tab[3][:].indirect(k_list[:, 16 * h : 16 * h + 16]))
-        for h in range(2):
-            cols = slice(h * HALF, (h + 1) * HALF)
-            nc.vector.tensor_tensor(out=u_rows[:, 3, cols], in0=k_last[h][:], in1=r_got[:, 3, cols], op=ADD)
-
-        res = {h: keep.tile([P, QT, W], F32, name="res%d" % h)[:] for h in (0, 3)}
+        res = [keep.tile([P, QT, HALF], F32, name="res%d" % a) for a in range(2)]
         out_rows = out[0].rearrange("(c p) n -> p c n", c=QT)
 
-        def product(h, c, eng):
-            acc = psum.tile([P, W], F32, name="acc%d%d" % (h, c))
+        def product(acc, h, c):
             nc.tensor.matmul_mx(
-                out=acc[:],
+                out=acc,
                 lhsT=q_codes[c][:].bitcast(FP8X4),
                 lhsT_scale=q_scales[c][:],
-                rhs=u_codes[h][:].bitcast(FP8X4),
+                rhs=u_codes[h].bitcast(FP8X4),
                 rhs_scale=u_scales[h][:],
                 start=True,
                 stop=True,
             )
-            if eng == "v":
-                nc.vector.tensor_scalar(out=res[h][:, c, :], in0=acc[:], scalar1=bias[:, c : c + 1], scalar2=None, op0=ADD)
-            else:
-                nc.scalar.activation(out=res[h][:, c, :], in_=acc[:], func=IDENTITY, bias=bias[:, c : c + 1])
 
-        pack("v", 0, 2)
-        pack("v", 3, 2)
-        mid_words = keep.tile([P, 2, W, PACK], BF16, name="mid_words", tag="q_raw1", align_bytes=64)
-        for h in (1, 2):
-            u_words[h] = mid_words[:, h - 1, :, :]
-            nc.scalar.activation(
-                out=u_words[h],
-                in_=u_rows[:, :, h * W : (h + 1) * W].rearrange("p t n -> p n t"),
-                func=COPY,
-            )
+        for c in range(QT):
+            cast_q(c)
+        all_codes = keep.tile([P, CH, W], U32, name="all_codes", tag="q_raw", align_bytes=64)
+        for h in range(CH):
+            u_codes[h] = all_codes[:, h, :]
         quant_q(0)
-        quant_u(0, "q_words0")
+        quant_u(0)
+        quant_u(1)
         quant_q(1)
-        quant_u(3, "u_words0")
-        quant_u(1, "q_words1")
-        quant_u(2, "u_words3")
-        mid_res = keep.tile([P, 2, QT, W], F32, name="mid_res", tag="q_raw1", align_bytes=64)
-        for h in (1, 2):
-            res[h] = mid_res[:, h - 1, :, :]
-        for h in (0, 3, 1, 2):
-            cols = slice(h * W, (h + 1) * W)
-            product(h, 0, "v" if h == 1 else "s")
-            product(h, 1, "s" if h in (0, 3) else "v")
-            if h != 2:
-                nc.sync.dma_start(out=out_rows[:, :, cols], in_=res[h])
+        quant_u(2)
+        quant_u(3)
+
+        def store(a, c, eng):
+            eng.dma_start(out=out_rows[:, c, a * HALF : (a + 1) * HALF], in_=res[a][:, c, :])
+
+        def leave(dst, acc, c, eng):
+            if eng == "v":
+                nc.vector.tensor_scalar(out=dst, in0=acc, scalar1=bias[:, c : c + 1], scalar2=None, op0=ADD)
             else:
-                nc.scalar.dma_start(out=out_rows[:, 0, cols], in_=res[h][:, 0, :])
-                nc.sync.dma_start(out=out_rows[:, 1, cols], in_=res[h][:, 1, :])
+                nc.scalar.activation(out=dst, in_=acc, func=IDENTITY, bias=bias[:, c : c + 1])
+
+        for c in range(QT):
+            acc = psum.tile([P, HALF], F32, name="acc_first%d" % c)
+            for h in range(2):
+                product(acc[:, h * W : (h + 1) * W], h, c)
+            leave(res[0][:, c, :], acc[:], c, "s")
+            store(0, c, nc.sync)
+        for h in (2, 3):
+            for c in range(QT):
+                acc = psum.tile([P, W], F32, name="acc%d%d" % (h, c))
+                product(acc[:], h, c)
+                leave(res[1][:, c, (h - 2) * W : (h - 1) * W], acc[:], c, "s" if c == 0 else "v")
+        store(1, 0, nc.scalar)
+        store(1, 1, nc.sync)

@@ -1,7 +1,6 @@
 from contextlib import ExitStack
 
 import concourse.mybir as mybir
-from concourse.masks import make_identity
 
 N, T, R, D, NQ = 512, 2048, 1024, 512, 256
 FLOPS = 2 * D * NQ * N
@@ -37,21 +36,19 @@ def tile_attend_pre_transe_f_topk_kernel(tc, qT, kT, rT, qn, offs, offs2, out):
         k_tab = [keep.tile([P, T], F32, name="k_tab%d" % t) for t in range(PACK)]
         r_tab = keep.tile([P, PACK, R], F32, name="r_tab")
         q_raw = keep.tile([P, PACK, NQ], F32, name="q_raw", align_bytes=64)
-        qn_rows = keep.tile([P, P], F32, name="qn_rows")
-        ident = keep.tile([P, P], F32, name="ident")
-        nc.vector.memset(qn_rows[:], 0.0)
-        make_identity(nc, ident[:])
+        qn_raw = keep.tile([P, QT], F32, name="qn_raw")
 
         nc.sync.dma_start(out=r_tab[:, 0, :], in_=r_rows[:, 0, :])
         nc.sync.dma_start(r_list[:], offs2)
         nc.sync.dma_start(k_list[:], offs)
         nc.sync.dma_start(out=r_tab[:, 1:3, :], in_=r_rows[:, 1:3, :])
         nc.sync.dma_start(out=k_tab[0][:], in_=k_rows[:, 0, :])
-        nc.sync.dma_start(out=qn_rows[0:QT, :], in_=qn[0].rearrange("(c p) o -> c (p o)", c=QT))
         nc.sync.dma_start(out=r_tab[:, 3, :], in_=r_rows[:, 3, :])
         for t in range(1, PACK):
             nc.sync.dma_start(out=k_tab[t][:], in_=k_rows[:, t, :])
         nc.sync.dma_start(out=q_raw[:], in_=qT[0].rearrange("(p t) q -> p t q", t=PACK))
+        with nc.allow_non_contiguous_dma(reason="one squared length a partition and query tile"):
+            nc.sync.dma_start(out=qn_raw[:], in_=qn[0].rearrange("(c p) o -> p (c o)", c=QT))
 
         k_got = keep.tile([P, PACK - 1, N], F32, name="k_got")
         r_got = keep.tile([P, PACK, N], F32, name="r_got")
@@ -102,10 +99,6 @@ def tile_attend_pre_transe_f_topk_kernel(tc, qT, kT, rT, qn, offs, offs2, out):
                 out=u_codes[h].bitcast(FP8X4), scales=u_scales[h][:], in_=u_words[h][:].rearrange("p n t -> p (n t)")
             )
 
-        qn_cols = psum.tile([P, P], F32, name="qn_cols", tag="turn")
-        nc.tensor.transpose(qn_cols[:], qn_rows[:], ident[:])
-        nc.scalar.activation(out=bias[:], in_=qn_cols[:, 0:QT], func=COPY, scale=-0.5)
-
         gather_r(0)
         gather_r(1)
         gather_r(2)
@@ -127,6 +120,7 @@ def tile_attend_pre_transe_f_topk_kernel(tc, qT, kT, rT, qn, offs, offs2, out):
             nc.vector.tensor_tensor(out=u_rows[:, 3, cols], in0=got, in1=r_got[:, 3, cols], op=ADD)
             pack("s", h, 2, rows(h, 2, 4))
 
+        nc.scalar.activation(out=bias[:], in_=qn_raw[:], func=COPY, scale=-0.5)
         res = [keep.tile([P, QT, HALF], F32, name="res%d" % a) for a in range(2)]
         out_rows = out[0].rearrange("(c p) n -> p c n", c=QT)
 

@@ -114,10 +114,10 @@ def tile_attend_pre_transe_f_topk_kernel(tc, qT, kT, rT, qn, offs, offs2, out):
 
         for a in range(2):
             nc.vector.tensor_copy(out=k_last[a][:], in_=k_tab[3][:].indirect(k_list[:, 16 * a : 16 * a + 16]))
+        for lo, hi in ((0, W), (W, HALF), (HALF, N)):
+            got = k_last[lo // HALF][:, lo % HALF : (hi - 1) % HALF + 1]
+            nc.vector.tensor_tensor(out=u_rows[:, 3, lo:hi], in0=got, in1=r_got[:, 3, lo:hi], op=ADD)
         for h in range(CH):
-            cols = slice(h * W, (h + 1) * W)
-            got = k_last[h // 2][:, (h % 2) * W : (h % 2 + 1) * W]
-            nc.vector.tensor_tensor(out=u_rows[:, 3, cols], in0=got, in1=r_got[:, 3, cols], op=ADD)
             pack("s", h, 2, rows(h, 2, 4))
 
         nc.scalar.activation(out=bias[:], in_=qn_raw[:], func=COPY, scale=-0.5)
@@ -156,16 +156,10 @@ def tile_attend_pre_transe_f_topk_kernel(tc, qT, kT, rT, qn, offs, offs2, out):
             else:
                 nc.scalar.activation(out=dst, in_=acc, func=IDENTITY, bias=bias[:, c : c + 1])
 
-        for c in range(QT):
-            acc = psum.tile([P, HALF], F32, name="acc_first%d" % c)
-            for h in range(2):
-                product(acc[:, h * W : (h + 1) * W], h, c)
-            leave(res[0][:, c, :], acc[:], c, "s")
-            store(0, c, nc.sync)
-        for h in (2, 3):
+        for a in range(2):
             for c in range(QT):
-                acc = psum.tile([P, W], F32, name="acc%d%d" % (h, c))
-                product(acc[:], h, c)
-                leave(res[1][:, c, (h - 2) * W : (h - 1) * W], acc[:], c, "s" if c == 0 else "v")
-        store(1, 0, nc.scalar)
-        store(1, 1, nc.sync)
+                for h in (2 * a, 2 * a + 1):
+                    acc = psum.tile([P, W], F32, name="acc%d%d" % (h, c))
+                    product(acc[:], h, c)
+                    leave(res[a][:, c, (h % 2) * W : (h % 2 + 1) * W], acc[:], c, "v" if (a, c) == (1, 1) else "s")
+                store(a, c, nc.scalar if a != c else nc.sync)

@@ -35,7 +35,10 @@ def tile_attend_pre_transe_f_topk_kernel(tc, qT, kT, rT, qn, offs, offs2, out):
         r_rows = rT.rearrange("(p t) n -> p t n", t=PACK)
         k_tab = [keep.tile([P, T], F32, name="k_tab%d" % t) for t in range(PACK)]
         r_tab = keep.tile([P, PACK, R], F32, name="r_tab")
-        q_raw = keep.tile([P, PACK, NQ], F32, name="q_raw", align_bytes=64)
+        q_first = keep.tile([P, PACK, P], F32, name="q_first", align_bytes=64)
+        q_raw = keep.tile([P, PACK, P], F32, name="q_raw", align_bytes=64)
+        q_tiles = [q_first, q_raw]
+        q_rows = qT[0].rearrange("(p t) q -> p t q", t=PACK)
         qn_raw = keep.tile([P, QT], F32, name="qn_raw")
 
         nc.sync.dma_start(out=r_tab[:, 0, :], in_=r_rows[:, 0, :])
@@ -46,7 +49,8 @@ def tile_attend_pre_transe_f_topk_kernel(tc, qT, kT, rT, qn, offs, offs2, out):
         nc.sync.dma_start(out=r_tab[:, 3, :], in_=r_rows[:, 3, :])
         for t in range(1, PACK):
             nc.sync.dma_start(out=k_tab[t][:], in_=k_rows[:, t, :])
-        nc.sync.dma_start(out=q_raw[:], in_=qT[0].rearrange("(p t) q -> p t q", t=PACK))
+        for c in range(QT):
+            nc.sync.dma_start(out=q_tiles[c][:], in_=q_rows[:, :, c * P : (c + 1) * P])
         with nc.allow_non_contiguous_dma(reason="one squared length a partition and query tile"):
             nc.sync.dma_start(out=qn_raw[:], in_=qn[0].rearrange("(c p) o -> p (c o)", c=QT))
 
@@ -70,9 +74,10 @@ def tile_attend_pre_transe_f_topk_kernel(tc, qT, kT, rT, qn, offs, offs2, out):
         def add(t):
             nc.vector.tensor_tensor(out=u_rows[:, t, :], in0=k_got[:, t, :], in1=r_got[:, t, :], op=ADD)
 
-        def pack(eng, h, lo, src):
+        def pack(eng, h, lo, src, first=0, last=W):
             planes = src.shape[1]
-            dst = u_words[h][:, :, lo : lo + planes]
+            src = src[:, :, first:last]
+            dst = u_words[h][:, first:last, lo : lo + planes]
             if eng == "v":
                 nc.vector.tensor_copy(out=dst, in_=src.rearrange("p t n -> p n t"))
             else:
@@ -81,11 +86,13 @@ def tile_attend_pre_transe_f_topk_kernel(tc, qT, kT, rT, qn, offs, offs2, out):
         def rows(h, lo, hi):
             return u_rows[:, lo:hi, h * W : (h + 1) * W]
 
-        def cast_q(c):
-            nc.vector.tensor_copy(
-                out=q_words[c][:].rearrange("p (g i) t -> p g t i", i=2),
-                in_=q_raw[:, :, c * P : (c + 1) * P].rearrange("p t (g i) -> p g t i", i=2),
-            )
+        def cast_q(c, eng):
+            dst = q_words[c][:].rearrange("p (g i) t -> p g t i", i=2)
+            src = q_tiles[c][:].rearrange("p t (g i) -> p g t i", i=2)
+            if eng == "v":
+                nc.vector.tensor_copy(out=dst, in_=src)
+            else:
+                nc.scalar.activation(out=dst, in_=src, func=COPY)
 
         def quant_q(c):
             nc.vector.quantize_mx(
@@ -112,12 +119,15 @@ def tile_attend_pre_transe_f_topk_kernel(tc, qT, kT, rT, qn, offs, offs2, out):
         gather_k(2)
         add(2)
 
+        cast_q(0, "s")
         for a in range(2):
             nc.vector.tensor_copy(out=k_last[a][:], in_=k_tab[3][:].indirect(k_list[:, 16 * a : 16 * a + 16]))
         for lo, hi in ((0, W), (W, HALF), (HALF, N)):
             got = k_last[lo // HALF][:, lo % HALF : (hi - 1) % HALF + 1]
             nc.vector.tensor_tensor(out=u_rows[:, 3, lo:hi], in0=got, in1=r_got[:, 3, lo:hi], op=ADD)
-        for h in range(CH):
+        pack("s", 0, 2, rows(0, 2, 4), 0, W // 2)
+        pack("v", 0, 2, rows(0, 2, 4), W // 2, W)
+        for h in range(1, CH):
             pack("s", h, 2, rows(h, 2, 4))
 
         nc.scalar.activation(out=bias[:], in_=qn_raw[:], func=COPY, scale=-0.5)
@@ -135,8 +145,7 @@ def tile_attend_pre_transe_f_topk_kernel(tc, qT, kT, rT, qn, offs, offs2, out):
                 stop=True,
             )
 
-        for c in range(QT):
-            cast_q(c)
+        cast_q(1, "v")
         all_codes = keep.tile([P, CH, W], U32, name="all_codes", tag="q_raw", align_bytes=64)
         for h in range(CH):
             u_codes[h] = all_codes[:, h, :]

@@ -21,6 +21,8 @@ HALF = N // 2
 QT = NQ // P
 W = 128
 CH = N // W
+Q_FIRST = 128
+V_PACK = 128
 
 
 def tile_attend_pre_transe_f_topk_kernel(tc, qT, kT, rT, qn, offs, offs2, out):
@@ -33,12 +35,13 @@ def tile_attend_pre_transe_f_topk_kernel(tc, qT, kT, rT, qn, offs, offs2, out):
         r_list = keep.tile([P, N // 16], U16, name="r_list")
         k_rows = kT.rearrange("(p t) n -> p t n", t=PACK)
         r_rows = rT.rearrange("(p t) n -> p t n", t=PACK)
+        q_rows = qT[0].rearrange("(p t) q -> p t q", t=PACK)
         k_tab = [keep.tile([P, T], F32, name="k_tab%d" % t) for t in range(PACK)]
         r_tab = keep.tile([P, PACK, R], F32, name="r_tab")
-        q_first = keep.tile([P, PACK, P], F32, name="q_first", align_bytes=64)
-        q_raw = keep.tile([P, PACK, P], F32, name="q_raw", align_bytes=64)
-        q_tiles = [q_first, q_raw]
-        q_rows = qT[0].rearrange("(p t) q -> p t q", t=PACK)
+        shared = keep.tile([P, N + 2 * PACK * Q_FIRST], BF16, name="shared", align_bytes=64)
+        q_first = shared[:, N:].bitcast(F32).rearrange("p (t q) -> p t q", t=PACK)
+        u_late = shared[:, : 2 * N].rearrange("p (t n) -> p t n", t=2)
+        q_rest = keep.tile([P, PACK, NQ - Q_FIRST], F32, name="q_rest", align_bytes=64)
         qn_raw = keep.tile([P, QT], F32, name="qn_raw")
 
         nc.sync.dma_start(out=r_tab[:, 0, :], in_=r_rows[:, 0, :])
@@ -49,21 +52,19 @@ def tile_attend_pre_transe_f_topk_kernel(tc, qT, kT, rT, qn, offs, offs2, out):
         nc.sync.dma_start(out=r_tab[:, 3, :], in_=r_rows[:, 3, :])
         for t in range(1, PACK):
             nc.sync.dma_start(out=k_tab[t][:], in_=k_rows[:, t, :])
-        for c in range(QT):
-            nc.sync.dma_start(out=q_tiles[c][:], in_=q_rows[:, :, c * P : (c + 1) * P])
+        nc.sync.dma_start(out=q_first, in_=q_rows[:, :, :Q_FIRST])
+        nc.sync.dma_start(out=q_rest[:], in_=q_rows[:, :, Q_FIRST:])
         with nc.allow_non_contiguous_dma(reason="one squared length a partition and query tile"):
             nc.sync.dma_start(out=qn_raw[:], in_=qn[0].rearrange("(c p) o -> p (c o)", c=QT))
 
         k_got = keep.tile([P, PACK - 1, N], F32, name="k_got")
         r_got = keep.tile([P, PACK, N], F32, name="r_got")
-        k_last = [keep.tile([P, HALF], F32, name="k_last%d" % a) for a in range(2)]
-        u_rows = keep.tile([P, PACK, N], BF16, name="u_rows")
+        k_last = [keep.tile([P, HALF], F32, name="k_last%d" % a, align_bytes=64) for a in range(2)]
+        u_early = keep.tile([P, 2, N], BF16, name="u_early")
         u_words = [keep.tile([P, W, PACK], BF16, name="u_words%d" % h, align_bytes=64) for h in range(CH)]
         u_scales = [keep.tile([P, W], U8, name="u_scales%d" % h, align_bytes=64) for h in range(CH)]
         q_words = [keep.tile([P, P, PACK], BF16, name="q_words%d" % c, align_bytes=64) for c in range(QT)]
-        q_codes = [keep.tile([P, P], U32, name="q_codes%d" % c, align_bytes=64) for c in range(QT)]
         q_scales = [keep.tile([P, P], U8, name="q_scales%d" % c, align_bytes=64) for c in range(QT)]
-        bias = keep.tile([P, QT], F32, name="bias")
 
         def gather_r(t):
             nc.vector.tensor_copy(out=r_got[:, t, :], in_=r_tab[:, t, :].indirect(r_list[:]))
@@ -71,90 +72,89 @@ def tile_attend_pre_transe_f_topk_kernel(tc, qT, kT, rT, qn, offs, offs2, out):
         def gather_k(t):
             nc.vector.tensor_copy(out=k_got[:, t, :], in_=k_tab[t][:].indirect(k_list[:]))
 
-        def add(t):
-            nc.vector.tensor_tensor(out=u_rows[:, t, :], in0=k_got[:, t, :], in1=r_got[:, t, :], op=ADD)
+        def add(dst, k_cols, r_cols):
+            nc.vector.tensor_tensor(out=dst, in0=k_cols, in1=r_cols, op=ADD)
 
-        def pack(eng, h, lo, src, first=0, last=W):
-            planes = src.shape[1]
-            src = src[:, :, first:last]
-            dst = u_words[h][:, first:last, lo : lo + planes]
-            if eng == "v":
-                nc.vector.tensor_copy(out=dst, in_=src.rearrange("p t n -> p n t"))
-            else:
-                nc.scalar.activation(out=dst, in_=src.rearrange("p t n -> p n t"), func=COPY)
+        def pack_early(h):
+            src = u_early[:, :, h * W : (h + 1) * W]
+            nc.scalar.activation(out=u_words[h][:, :, 0:2], in_=src.rearrange("p t n -> p n t"), func=COPY)
 
-        def rows(h, lo, hi):
-            return u_rows[:, lo:hi, h * W : (h + 1) * W]
-
-        def cast_q(c, eng):
-            dst = q_words[c][:].rearrange("p (g i) t -> p g t i", i=2)
-            src = q_tiles[c][:].rearrange("p t (g i) -> p g t i", i=2)
+        def pack_late(eng, lo, hi):
+            h = lo // W
+            dst = u_words[h][:, lo - h * W : hi - h * W, 2:4]
+            src = u_late[:, :, lo:hi].rearrange("p t n -> p n t")
             if eng == "v":
                 nc.vector.tensor_copy(out=dst, in_=src)
             else:
                 nc.scalar.activation(out=dst, in_=src, func=COPY)
 
-        def quant_q(c):
-            nc.vector.quantize_mx(
-                out=q_codes[c][:].bitcast(FP8X4), scales=q_scales[c][:], in_=q_words[c][:].rearrange("p m t -> p (m t)")
-            )
+        def cast_q(eng, raw, first, lo, hi):
+            c = lo // P
+            dst = q_words[c][:, lo - c * P : hi - c * P, :].rearrange("p (g i) t -> p g t i", i=2)
+            src = raw[:, :, lo - first : hi - first].rearrange("p t (g i) -> p g t i", i=2)
+            if eng == "v":
+                nc.vector.tensor_copy(out=dst, in_=src)
+            else:
+                nc.scalar.activation(out=dst, in_=src, func=COPY)
 
-        u_codes = {}
-
-        def quant_u(h):
-            nc.vector.quantize_mx(
-                out=u_codes[h].bitcast(FP8X4), scales=u_scales[h][:], in_=u_words[h][:].rearrange("p n t -> p (n t)")
-            )
+        def quantise(codes, scales, words):
+            nc.vector.quantize_mx(out=codes.bitcast(FP8X4), scales=scales[:], in_=words[:].rearrange("p m t -> p (m t)"))
 
         gather_r(0)
         gather_r(1)
         gather_r(2)
         gather_k(0)
         gather_r(3)
-        add(0)
+        add(u_early[:, 0, :], k_got[:, 0, :], r_got[:, 0, :])
         gather_k(1)
-        add(1)
+        add(u_early[:, 1, :], k_got[:, 1, :], r_got[:, 1, :])
         for h in range(CH):
-            pack("s", h, 0, rows(h, 0, 2))
+            pack_early(h)
         gather_k(2)
-        add(2)
+        add(u_late[:, 0, :], k_got[:, 2, :], r_got[:, 2, :])
 
-        cast_q(0, "s")
+        cast_q("s", q_first, 0, 0, P // 2)
+        cast_q("s", q_first, 0, P // 2, P)
+        cast_q("s", q_rest, Q_FIRST, Q_FIRST, NQ)
         for a in range(2):
             nc.vector.tensor_copy(out=k_last[a][:], in_=k_tab[3][:].indirect(k_list[:, 16 * a : 16 * a + 16]))
         for lo, hi in ((0, W), (W, HALF), (HALF, N)):
-            got = k_last[lo // HALF][:, lo % HALF : (hi - 1) % HALF + 1]
-            nc.vector.tensor_tensor(out=u_rows[:, 3, lo:hi], in0=got, in1=r_got[:, 3, lo:hi], op=ADD)
-        pack("s", 0, 2, rows(0, 2, 4), 0, W // 2)
-        pack("v", 0, 2, rows(0, 2, 4), W // 2, W)
-        for h in range(1, CH):
-            pack("s", h, 2, rows(h, 2, 4))
-
+            cols = slice(lo % HALF, (hi - 1) % HALF + 1)
+            add(u_late[:, 1, lo:hi], k_last[lo // HALF][:, cols], r_got[:, 3, lo:hi])
+        pack_late("s", 0, W)
+        pack_late("v", W, W + V_PACK)
+        bias = keep.tile([P, QT], F32, name="bias", tag="k_last0", align_bytes=64)
         nc.scalar.activation(out=bias[:], in_=qn_raw[:], func=COPY, scale=-0.5)
+        for h in range(2, CH):
+            pack_late("s", h * W, (h + 1) * W)
+
         res = [keep.tile([P, QT, HALF], F32, name="res%d" % a) for a in range(2)]
         out_rows = out[0].rearrange("(c p) n -> p c n", c=QT)
 
-        def product(acc, h, c):
+        u_all = keep.tile([P, CH, W], U32, name="u_all", align_bytes=64)
+        u_codes = [u_all[:, h, :] for h in range(CH)]
+        q_codes0 = keep.tile([P, P], U32, name="q_codes0", tag="k_last1", align_bytes=64)
+        q_codes1 = keep.tile([P, P], U32, name="q_codes1", align_bytes=64)
+        q_codes = [q_codes0[:], q_codes1[:]]
+        quantise(q_codes[0], q_scales[0], q_words[0])
+        quantise(u_codes[1], u_scales[1], u_words[1])
+        quantise(u_codes[0], u_scales[0], u_words[0])
+        quantise(q_codes[1], q_scales[1], q_words[1])
+        quantise(u_codes[2], u_scales[2], u_words[2])
+        quantise(u_codes[3], u_scales[3], u_words[3])
+
+        def product(h, c):
+            acc = psum.tile([P, W], F32, name="acc%d%d" % (h, c))
             nc.tensor.matmul_mx(
-                out=acc,
-                lhsT=q_codes[c][:].bitcast(FP8X4),
+                out=acc[:],
+                lhsT=q_codes[c].bitcast(FP8X4),
                 lhsT_scale=q_scales[c][:],
                 rhs=u_codes[h].bitcast(FP8X4),
                 rhs_scale=u_scales[h][:],
                 start=True,
                 stop=True,
             )
-
-        cast_q(1, "v")
-        all_codes = keep.tile([P, CH, W], U32, name="all_codes", tag="q_raw", align_bytes=64)
-        for h in range(CH):
-            u_codes[h] = all_codes[:, h, :]
-        quant_q(0)
-        quant_u(0)
-        quant_u(1)
-        quant_q(1)
-        quant_u(2)
-        quant_u(3)
+            return acc
 
         def store(a, c, eng):
             eng.dma_start(out=out_rows[:, c, a * HALF : (a + 1) * HALF], in_=res[a][:, c, :])
@@ -165,10 +165,9 @@ def tile_attend_pre_transe_f_topk_kernel(tc, qT, kT, rT, qn, offs, offs2, out):
             else:
                 nc.scalar.activation(out=dst, in_=acc, func=IDENTITY, bias=bias[:, c : c + 1])
 
-        for a in range(2):
+        for a, chunks in enumerate(((1, 0), (2, 3))):
             for c in range(QT):
-                for h in (2 * a, 2 * a + 1):
-                    acc = psum.tile([P, W], F32, name="acc%d%d" % (h, c))
-                    product(acc[:], h, c)
+                for h in chunks:
+                    acc = product(h, c)
                     leave(res[a][:, c, (h % 2) * W : (h % 2 + 1) * W], acc[:], c, "v" if (a, c) == (1, 1) else "s")
                 store(a, c, nc.scalar if a != c else nc.sync)

@@ -22,6 +22,7 @@ QT = NQ // P
 W = 128
 CH = N // W
 Q_FIRST = 128
+S_CAST = 64
 V_PACK = 128
 
 
@@ -59,11 +60,14 @@ def tile_attend_pre_transe_f_topk_kernel(tc, qT, kT, rT, qn, offs, offs2, out):
 
         k_got = keep.tile([P, PACK - 1, N], F32, name="k_got")
         r_got = keep.tile([P, PACK, N], F32, name="r_got")
-        k_last = [keep.tile([P, HALF], F32, name="k_last%d" % a, align_bytes=64) for a in range(2)]
+        second = keep.tile([P, PACK * S_CAST + N], BF16, name="second", align_bytes=64)
+        k_last1 = keep.tile([P, HALF], F32, name="k_last1", align_bytes=64)
+        k_last = [second[:, PACK * S_CAST :].bitcast(F32), k_last1[:]]
         u_early = keep.tile([P, 2, N], BF16, name="u_early")
         u_words = [keep.tile([P, W, PACK], BF16, name="u_words%d" % h, align_bytes=64) for h in range(CH)]
         u_scales = [keep.tile([P, W], U8, name="u_scales%d" % h, align_bytes=64) for h in range(CH)]
-        q_words = [keep.tile([P, P, PACK], BF16, name="q_words%d" % c, align_bytes=64) for c in range(QT)]
+        q_words0 = keep.tile([P, P, PACK], BF16, name="q_words0", align_bytes=64)
+        q_words = [q_words0[:], second[:, : PACK * P].rearrange("p (m t) -> p m t", t=PACK)]
         q_scales = [keep.tile([P, P], U8, name="q_scales%d" % c, align_bytes=64) for c in range(QT)]
 
         def gather_r(t):
@@ -98,7 +102,7 @@ def tile_attend_pre_transe_f_topk_kernel(tc, qT, kT, rT, qn, offs, offs2, out):
                 nc.scalar.activation(out=dst, in_=src, func=COPY)
 
         def quantise(codes, scales, words):
-            nc.vector.quantize_mx(out=codes.bitcast(FP8X4), scales=scales[:], in_=words[:].rearrange("p m t -> p (m t)"))
+            nc.vector.quantize_mx(out=codes.bitcast(FP8X4), scales=scales[:], in_=words.rearrange("p m t -> p (m t)"))
 
         gather_r(0)
         gather_r(1)
@@ -115,18 +119,19 @@ def tile_attend_pre_transe_f_topk_kernel(tc, qT, kT, rT, qn, offs, offs2, out):
 
         cast_q("s", q_first, 0, 0, P // 2)
         cast_q("s", q_first, 0, P // 2, P)
-        cast_q("s", q_rest, Q_FIRST, Q_FIRST, NQ)
+        cast_q("s", q_rest, Q_FIRST, P, P + S_CAST)
         for a in range(2):
-            nc.vector.tensor_copy(out=k_last[a][:], in_=k_tab[3][:].indirect(k_list[:, 16 * a : 16 * a + 16]))
+            nc.vector.tensor_copy(out=k_last[a], in_=k_tab[3][:].indirect(k_list[:, 16 * a : 16 * a + 16]))
         for lo, hi in ((0, W), (W, HALF), (HALF, N)):
             cols = slice(lo % HALF, (hi - 1) % HALF + 1)
             add(u_late[:, 1, lo:hi], k_last[lo // HALF][:, cols], r_got[:, 3, lo:hi])
         pack_late("s", 0, W)
         pack_late("v", W, W + V_PACK)
-        bias = keep.tile([P, QT], F32, name="bias", tag="k_last0", align_bytes=64)
+        cast_q("v", q_rest, Q_FIRST, P + S_CAST, NQ)
+        pack_late("s", 2 * W, 3 * W)
+        bias = keep.tile([P, QT], F32, name="bias", tag="q_rest", align_bytes=64)
         nc.scalar.activation(out=bias[:], in_=qn_raw[:], func=COPY, scale=-0.5)
-        for h in range(2, CH):
-            pack_late("s", h * W, (h + 1) * W)
+        pack_late("s", 3 * W, N)
 
         res = [keep.tile([P, QT, HALF], F32, name="res%d" % a) for a in range(2)]
         out_rows = out[0].rearrange("(c p) n -> p c n", c=QT)
@@ -137,11 +142,11 @@ def tile_attend_pre_transe_f_topk_kernel(tc, qT, kT, rT, qn, offs, offs2, out):
         q_codes1 = keep.tile([P, P], U32, name="q_codes1", align_bytes=64)
         q_codes = [q_codes0[:], q_codes1[:]]
         quantise(q_codes[0], q_scales[0], q_words[0])
-        quantise(u_codes[1], u_scales[1], u_words[1])
-        quantise(u_codes[0], u_scales[0], u_words[0])
+        quantise(u_codes[1], u_scales[1], u_words[1][:])
+        quantise(u_codes[0], u_scales[0], u_words[0][:])
         quantise(q_codes[1], q_scales[1], q_words[1])
-        quantise(u_codes[2], u_scales[2], u_words[2])
-        quantise(u_codes[3], u_scales[3], u_words[3])
+        quantise(u_codes[2], u_scales[2], u_words[2][:])
+        quantise(u_codes[3], u_scales[3], u_words[3][:])
 
         def product(h, c):
             acc = psum.tile([P, W], F32, name="acc%d%d" % (h, c))

@@ -41,7 +41,7 @@ def tile_attend_pre_transe_f_topk_kernel(tc, qT, kT, rT, qn, offs, offs2, out):
         r_tab = keep.tile([P, PACK, R], F32, name="r_tab")
         shared = keep.tile([P, N + 2 * PACK * Q_FIRST], BF16, name="shared", align_bytes=64)
         q_first = shared[:, N:].bitcast(F32).rearrange("p (t q) -> p t q", t=PACK)
-        u_late = shared[:, : 2 * N].rearrange("p (t n) -> p t n", t=2)
+        blocks = shared[:].rearrange("p (b n) -> p b n", n=W)
         q_rest = keep.tile([P, PACK, NQ - Q_FIRST], F32, name="q_rest", align_bytes=64)
         qn_raw = keep.tile([P, QT], F32, name="qn_raw")
 
@@ -86,7 +86,7 @@ def tile_attend_pre_transe_f_topk_kernel(tc, qT, kT, rT, qn, offs, offs2, out):
         def pack_late(eng, lo, hi):
             h = lo // W
             dst = u_words[h][:, lo - h * W : hi - h * W, 2:4]
-            src = u_late[:, :, lo:hi].rearrange("p t n -> p n t")
+            src = blocks[:, h : CH + 2 * h + 1 : CH + h, lo - h * W : hi - h * W].rearrange("p t n -> p n t")
             if eng == "v":
                 nc.vector.tensor_copy(out=dst, in_=src)
             else:
@@ -115,7 +115,7 @@ def tile_attend_pre_transe_f_topk_kernel(tc, qT, kT, rT, qn, offs, offs2, out):
         for h in range(CH):
             pack_early(h)
         gather_k(2)
-        add(u_late[:, 0, :], k_got[:, 2, :], r_got[:, 2, :])
+        add(shared[:, :N], k_got[:, 2, :], r_got[:, 2, :])
 
         cast_q("s", q_first, 0, 0, P // 2)
         cast_q("s", q_first, 0, P // 2, P)
@@ -124,7 +124,11 @@ def tile_attend_pre_transe_f_topk_kernel(tc, qT, kT, rT, qn, offs, offs2, out):
             nc.vector.tensor_copy(out=k_last[a], in_=k_tab[3][:].indirect(k_list[:, 16 * a : 16 * a + 16]))
         for lo, hi in ((0, W), (W, HALF), (HALF, N)):
             cols = slice(lo % HALF, (hi - 1) % HALF + 1)
-            add(u_late[:, 1, lo:hi], k_last[lo // HALF][:, cols], r_got[:, 3, lo:hi])
+            add(
+                blocks[:, CH + 2 * (lo // W) : CH + 2 * (hi // W) : 2, :],
+                k_last[lo // HALF][:, cols].rearrange("p (b n) -> p b n", n=W),
+                r_got[:, 3, lo:hi].rearrange("p (b n) -> p b n", n=W),
+            )
         pack_late("s", 0, W)
         pack_late("v", W, W + V_PACK)
         cast_q("v", q_rest, Q_FIRST, P + S_CAST, NQ)

@@ -178,5 +178,5 @@ def tile_attend_pre_transe_f_topk_kernel(tc, qT, kT, rT, qn, offs, offs2, out):
             for c in range(QT):
                 for h in chunks:
                     acc = product(h, c)
-                    leave(res[a][:, c, (h % 2) * W : (h % 2 + 1) * W], acc[:], c, "v" if (a, c) == (1, 1) else "s")
-                store(a, c, nc.scalar if a != c else nc.sync)
+                    leave(res[a][:, c, (h % 2) * W : (h % 2 + 1) * W], acc[:], c, "v" if a == 1 else "s")
+                store(a, c, nc.scalar if c == 1 else nc.sync)

@@ -21,9 +21,8 @@ HALF = N // 2
 QT = NQ // P
 W = 128
 CH = N // W
-Q_FIRST = 128
-S_CAST = 64
-V_PACK = 128
+S_CAST = 96
+I32 = mybir.dt.int32
 
 
 def tile_attend_pre_transe_f_topk_kernel(tc, qT, kT, rT, qn, offs, offs2, out):
@@ -37,136 +36,148 @@ def tile_attend_pre_transe_f_topk_kernel(tc, qT, kT, rT, qn, offs, offs2, out):
         k_rows = kT.rearrange("(p t) n -> p t n", t=PACK)
         r_rows = rT.rearrange("(p t) n -> p t n", t=PACK)
         q_rows = qT[0].rearrange("(p t) q -> p t q", t=PACK)
-        k_tab = [keep.tile([P, T], F32, name="k_tab%d" % t) for t in range(PACK)]
+        k_pair = keep.tile([P, 2, T], F32, name="k_pair")
+        k_tab = [k_pair[:, 0, :], k_pair[:, 1, :]] + [keep.tile([P, T], F32, name="k_tab%d" % t)[:] for t in (2, 3)]
         r_tab = keep.tile([P, PACK, R], F32, name="r_tab")
-        shared = keep.tile([P, N + 2 * PACK * Q_FIRST], BF16, name="shared", align_bytes=64)
+        shared = keep.tile([P, N + 2 * PACK * P], BF16, name="shared", align_bytes=64)
         q_first = shared[:, N:].bitcast(F32).rearrange("p (t q) -> p t q", t=PACK)
         blocks = shared[:].rearrange("p (b n) -> p b n", n=W)
-        q_rest = keep.tile([P, PACK, NQ - Q_FIRST], F32, name="q_rest", align_bytes=64)
+        q_rest = keep.tile([P, PACK, P], F32, name="q_rest", align_bytes=64)
         qn_raw = keep.tile([P, QT], F32, name="qn_raw")
 
-        nc.sync.dma_start(out=r_tab[:, 0, :], in_=r_rows[:, 0, :])
+        nc.sync.dma_start(out=r_tab[:], in_=r_rows)
         nc.sync.dma_start(r_list[:], offs2)
         nc.sync.dma_start(k_list[:], offs)
-        nc.sync.dma_start(out=r_tab[:, 1:3, :], in_=r_rows[:, 1:3, :])
-        nc.sync.dma_start(out=k_tab[0][:], in_=k_rows[:, 0, :])
-        nc.sync.dma_start(out=r_tab[:, 3, :], in_=r_rows[:, 3, :])
-        for t in range(1, PACK):
-            nc.sync.dma_start(out=k_tab[t][:], in_=k_rows[:, t, :])
-        nc.sync.dma_start(out=q_first, in_=q_rows[:, :, :Q_FIRST])
-        nc.sync.dma_start(out=q_rest[:], in_=q_rows[:, :, Q_FIRST:])
+        nc.sync.dma_start(out=k_pair[:], in_=k_rows[:, :2, :])
+        for t in (2, 3):
+            nc.sync.dma_start(out=k_tab[t], in_=k_rows[:, t, :])
+        nc.sync.dma_start(out=q_first, in_=q_rows[:, :, :P])
+        nc.sync.dma_start(out=q_rest[:], in_=q_rows[:, :, P:])
         with nc.allow_non_contiguous_dma(reason="one squared length a partition and query tile"):
             nc.sync.dma_start(out=qn_raw[:], in_=qn[0].rearrange("(c p) o -> p (c o)", c=QT))
 
         k_got = keep.tile([P, PACK - 1, N], F32, name="k_got")
         r_got = keep.tile([P, PACK, N], F32, name="r_got")
-        second = keep.tile([P, PACK * S_CAST + N], BF16, name="second", align_bytes=64)
-        k_last1 = keep.tile([P, HALF], F32, name="k_last1", align_bytes=64)
-        k_last = [second[:, PACK * S_CAST :].bitcast(F32), k_last1[:]]
-        u_early = keep.tile([P, 2, N], BF16, name="u_early")
-        u_words = [keep.tile([P, W, PACK], BF16, name="u_words%d" % h, align_bytes=64) for h in range(CH)]
+        k_last = [keep.tile([P, W], F32, name="k_last%d" % h, align_bytes=64) for h in range(CH)]
+        u_late = keep.tile([P, 2, W], BF16, name="u_late")
+        late = {0: u_late[:], 2: blocks[:, 2:5:2, :], 3: blocks[:, 3:7:3, :]}
+        u_pairs = keep.tile([P, 2, W, 2], BF16, name="u_pairs")
+        u_words = {h: keep.tile([P, W, PACK], BF16, name="u_words%d" % h, align_bytes=64) for h in late}
+        q_words = keep.tile([P, NQ, PACK], BF16, name="q_words", align_bytes=64)
+        u_codes = {}
         u_scales = [keep.tile([P, W], U8, name="u_scales%d" % h, align_bytes=64) for h in range(CH)]
-        q_words0 = keep.tile([P, P, PACK], BF16, name="q_words0", align_bytes=64)
-        q_words = [q_words0[:], second[:, : PACK * P].rearrange("p (m t) -> p m t", t=PACK)]
+        q_codes = [keep.tile([P, P], U32, name="q_codes%d" % c, align_bytes=64) for c in range(QT)]
         q_scales = [keep.tile([P, P], U8, name="q_scales%d" % c, align_bytes=64) for c in range(QT)]
+        bias = keep.tile([P, QT], F32, name="bias")
 
-        def gather_r(t):
-            nc.vector.tensor_copy(out=r_got[:, t, :], in_=r_tab[:, t, :].indirect(r_list[:]))
-
-        def gather_k(t):
-            nc.vector.tensor_copy(out=k_got[:, t, :], in_=k_tab[t][:].indirect(k_list[:]))
+        def move(eng, dst, src):
+            if eng == "v":
+                nc.vector.tensor_copy(out=dst, in_=src)
+            else:
+                nc.scalar.activation(out=dst, in_=src, func=COPY)
 
         def add(dst, k_cols, r_cols):
             nc.vector.tensor_tensor(out=dst, in0=k_cols, in1=r_cols, op=ADD)
 
-        def pack_early(h):
-            src = u_early[:, :, h * W : (h + 1) * W]
-            nc.scalar.activation(out=u_words[h][:, :, 0:2], in_=src.rearrange("p t n -> p n t"), func=COPY)
+        def slots(h):
+            return slice(h * W, (h + 1) * W)
 
-        def pack_late(eng, lo, hi):
-            h = lo // W
-            dst = u_words[h][:, lo - h * W : hi - h * W, 2:4]
-            src = blocks[:, h : CH + 2 * h + 1 : CH + h, lo - h * W : hi - h * W].rearrange("p t n -> p n t")
-            if eng == "v":
-                nc.vector.tensor_copy(out=dst, in_=src)
-            else:
-                nc.scalar.activation(out=dst, in_=src, func=COPY)
+        def add_early(h):
+            by_twos = "p t (g i) -> p g t i"
+            dst = u_words[h][:, :, 0:2] if h in late else u_pairs[:, 0, :, :]
+            add(
+                dst.rearrange("p (g i) t -> p g t i", i=2),
+                k_got[:, 0:2, slots(h)].rearrange(by_twos, i=2),
+                r_got[:, 0:2, slots(h)].rearrange(by_twos, i=2),
+            )
+
+        def pack(eng, h):
+            move(eng, u_words[h][:, :, 2:4], late[h].rearrange("p t n -> p n t"))
 
         def cast_q(eng, raw, first, lo, hi):
-            c = lo // P
-            dst = q_words[c][:, lo - c * P : hi - c * P, :].rearrange("p (g i) t -> p g t i", i=2)
+            dst = q_words[:, lo:hi, :].rearrange("p (g i) t -> p g t i", i=2)
             src = raw[:, :, lo - first : hi - first].rearrange("p t (g i) -> p g t i", i=2)
-            if eng == "v":
-                nc.vector.tensor_copy(out=dst, in_=src)
-            else:
-                nc.scalar.activation(out=dst, in_=src, func=COPY)
+            move(eng, dst, src)
+
+        def gather_r(eng, t):
+            move(eng, r_got[:, t, :], r_tab[:, t, :].indirect(r_list[:]))
+
+        def gather_k(eng, t, lo, hi):
+            move(eng, k_got[:, t, lo:hi], k_tab[t].indirect(k_list[:, lo // 16 : hi // 16]))
+
+        def gather_last(eng, h):
+            move(eng, k_last[h][:], k_tab[3].indirect(k_list[:, 8 * h : 8 * h + 8]))
+
+        def add_late(t, h, k_cols):
+            dst = late[h][:, t - 2, :] if h in late else u_pairs[:, 1, :, t - 2]
+            add(dst, k_cols, r_got[:, t, slots(h)])
+
+        def add_last(h):
+            add_late(3, h, k_last[h][:])
+
+        def weave(h, slot):
+            u_words.setdefault(h, keep.tile([P, W, PACK], BF16, name="u_words%d" % h, tag=slot, align_bytes=64))
+            src = u_pairs[:].rearrange("p j n e -> p j (n e)").bitcast(I32)
+            dst = u_words[h][:].rearrange("p n t -> p (n t)").bitcast(I32)
+            nc.vector.tensor_copy(out=dst.rearrange("p (n j) -> p n j", j=2), in_=src.rearrange("p j n -> p n j"))
 
         def quantise(codes, scales, words):
-            nc.vector.quantize_mx(out=codes.bitcast(FP8X4), scales=scales[:], in_=words.rearrange("p m t -> p (m t)"))
+            nc.vector.quantize_mx(out=codes.bitcast(FP8X4), scales=scales, in_=words.rearrange("p m t -> p (m t)"))
 
-        gather_r(0)
-        gather_r(1)
-        gather_r(2)
-        gather_k(0)
-        gather_r(3)
-        add(u_early[:, 0, :], k_got[:, 0, :], r_got[:, 0, :])
-        gather_k(1)
-        add(u_early[:, 1, :], k_got[:, 1, :], r_got[:, 1, :])
+        def quantise_u(h, slot):
+            u_codes.setdefault(h, keep.tile([P, W], U32, name="u_codes%d" % h, tag=slot, align_bytes=64))
+            quantise(u_codes[h][:], u_scales[h][:], u_words[h][:])
+
+        def quantise_q(c):
+            quantise(q_codes[c][:], q_scales[c][:], q_words[:, c * P : (c + 1) * P, :])
+
+        for t in range(PACK):
+            gather_r("vvvs"[t], t)
+        gather_k("v", 0, 0, N)
+        gather_k("s", 1, 0, N)
         for h in range(CH):
-            pack_early(h)
-        gather_k(2)
-        add(shared[:, :N], k_got[:, 2, :], r_got[:, 2, :])
+            add_early(h)
+        gather_k("s", 2, 0, N)
+        for h in range(CH):
+            add_late(2, h, k_got[:, 2, slots(h)])
 
+        for h in range(CH):
+            gather_last("vvss"[h], h)
         cast_q("s", q_first, 0, 0, P // 2)
         cast_q("s", q_first, 0, P // 2, P)
-        cast_q("s", q_rest, Q_FIRST, P, P + S_CAST)
-        for a in range(2):
-            nc.vector.tensor_copy(out=k_last[a], in_=k_tab[3][:].indirect(k_list[:, 16 * a : 16 * a + 16]))
-        for lo, hi in ((0, W), (W, HALF), (HALF, N)):
-            cols = slice(lo % HALF, (hi - 1) % HALF + 1)
-            add(
-                blocks[:, CH + 2 * (lo // W) : CH + 2 * (hi // W) : 2, :],
-                k_last[lo // HALF][:, cols].rearrange("p (b n) -> p b n", n=W),
-                r_got[:, 3, lo:hi].rearrange("p (b n) -> p b n", n=W),
-            )
-        pack_late("s", 0, W)
-        pack_late("v", W, W + V_PACK)
-        cast_q("v", q_rest, Q_FIRST, P + S_CAST, NQ)
-        pack_late("s", 2 * W, 3 * W)
-        bias = keep.tile([P, QT], F32, name="bias", tag="q_rest", align_bytes=64)
+        add_last(0)
+        add_last(1)
+        pack("v", 0)
+        add_last(2)
+        add_last(3)
+        pack("s", 2)
+        cast_q("s", q_rest, P, P, P + S_CAST)
+        pack("s", 3)
         nc.scalar.activation(out=bias[:], in_=qn_raw[:], func=COPY, scale=-0.5)
-        pack_late("s", 3 * W, N)
+        quantise_q(0)
+        quantise_u(0, "k_last3")
+        weave(1, "k_last2")
+        cast_q("v", q_rest, P, P + S_CAST, NQ)
+        quantise_u(1, "u_codes1")
+        quantise_q(1)
+        quantise_u(2, "u_codes2")
+        quantise_u(3, "u_codes3")
 
         res = [keep.tile([P, QT, HALF], F32, name="res%d" % a) for a in range(2)]
         out_rows = out[0].rearrange("(c p) n -> p c n", c=QT)
-
-        u_all = keep.tile([P, CH, W], U32, name="u_all", align_bytes=64)
-        u_codes = [u_all[:, h, :] for h in range(CH)]
-        q_codes0 = keep.tile([P, P], U32, name="q_codes0", tag="k_last1", align_bytes=64)
-        q_codes1 = keep.tile([P, P], U32, name="q_codes1", align_bytes=64)
-        q_codes = [q_codes0[:], q_codes1[:]]
-        quantise(q_codes[0], q_scales[0], q_words[0])
-        quantise(u_codes[1], u_scales[1], u_words[1][:])
-        quantise(u_codes[0], u_scales[0], u_words[0][:])
-        quantise(q_codes[1], q_scales[1], q_words[1])
-        quantise(u_codes[2], u_scales[2], u_words[2][:])
-        quantise(u_codes[3], u_scales[3], u_words[3][:])
 
         def product(h, c):
             acc = psum.tile([P, W], F32, name="acc%d%d" % (h, c))
             nc.tensor.matmul_mx(
                 out=acc[:],
-                lhsT=q_codes[c].bitcast(FP8X4),
+                lhsT=q_codes[c][:].bitcast(FP8X4),
                 lhsT_scale=q_scales[c][:],
-                rhs=u_codes[h].bitcast(FP8X4),
+                rhs=u_codes[h][:].bitcast(FP8X4),
                 rhs_scale=u_scales[h][:],
                 start=True,
                 stop=True,
             )
             return acc
-
-        def store(a, c, eng):
-            eng.dma_start(out=out_rows[:, c, a * HALF : (a + 1) * HALF], in_=res[a][:, c, :])
 
         def leave(dst, acc, c, eng):
             if eng == "v":
@@ -174,9 +185,12 @@ def tile_attend_pre_transe_f_topk_kernel(tc, qT, kT, rT, qn, offs, offs2, out):
             else:
                 nc.scalar.activation(out=dst, in_=acc, func=IDENTITY, bias=bias[:, c : c + 1])
 
-        for a, chunks in enumerate(((1, 0), (2, 3))):
+        def store(a, c):
+            eng = nc.scalar if c == 1 else nc.sync
+            eng.dma_start(out=out_rows[:, c, a * HALF : (a + 1) * HALF], in_=res[a][:, c, :])
+
+        for a in range(2):
             for c in range(QT):
-                for h in chunks:
-                    acc = product(h, c)
-                    leave(res[a][:, c, (h % 2) * W : (h % 2 + 1) * W], acc[:], c, "v" if a == 1 else "s")
-                store(a, c, nc.scalar if c == 1 else nc.sync)
+                for h in (2 * a, 2 * a + 1):
+                    leave(res[a][:, c, slots(h % 2)], product(h, c)[:], c, "v" if a == 1 else "s")
+                store(a, c)

@@ -36,8 +36,7 @@ def tile_attend_pre_transe_f_topk_kernel(tc, qT, kT, rT, qn, offs, offs2, out):
         k_rows = kT.rearrange("(p t) n -> p t n", t=PACK)
         r_rows = rT.rearrange("(p t) n -> p t n", t=PACK)
         q_rows = qT[0].rearrange("(p t) q -> p t q", t=PACK)
-        k_pair = keep.tile([P, 2, T], F32, name="k_pair")
-        k_tab = [k_pair[:, 0, :], k_pair[:, 1, :]] + [keep.tile([P, T], F32, name="k_tab%d" % t)[:] for t in (2, 3)]
+        k_tab = [keep.tile([P, T], F32, name="k_tab%d" % t) for t in range(PACK)]
         r_tab = keep.tile([P, PACK, R], F32, name="r_tab")
         shared = keep.tile([P, N + 2 * PACK * P], BF16, name="shared", align_bytes=64)
         q_first = shared[:, N:].bitcast(F32).rearrange("p (t q) -> p t q", t=PACK)
@@ -48,9 +47,8 @@ def tile_attend_pre_transe_f_topk_kernel(tc, qT, kT, rT, qn, offs, offs2, out):
         nc.sync.dma_start(out=r_tab[:], in_=r_rows)
         nc.sync.dma_start(r_list[:], offs2)
         nc.sync.dma_start(k_list[:], offs)
-        nc.sync.dma_start(out=k_pair[:], in_=k_rows[:, :2, :])
-        for t in (2, 3):
-            nc.sync.dma_start(out=k_tab[t], in_=k_rows[:, t, :])
+        for t in range(PACK):
+            nc.sync.dma_start(out=k_tab[t][:], in_=k_rows[:, t, :])
         nc.sync.dma_start(out=q_first, in_=q_rows[:, :, :P])
         nc.sync.dma_start(out=q_rest[:], in_=q_rows[:, :, P:])
         with nc.allow_non_contiguous_dma(reason="one squared length a partition and query tile"):
@@ -59,8 +57,8 @@ def tile_attend_pre_transe_f_topk_kernel(tc, qT, kT, rT, qn, offs, offs2, out):
         k_got = keep.tile([P, PACK - 1, N], F32, name="k_got")
         r_got = keep.tile([P, PACK, N], F32, name="r_got")
         k_last = [keep.tile([P, W], F32, name="k_last%d" % h, align_bytes=64) for h in range(CH)]
-        u_late = keep.tile([P, 2, W], BF16, name="u_late")
-        late = {0: u_late[:], 2: blocks[:, 2:5:2, :], 3: blocks[:, 3:7:3, :]}
+        u_early = keep.tile([P, 2, N], BF16, name="u_early")
+        late = {1: blocks[:, 0:4:3, :], 2: blocks[:, 1:5:3, :], 3: blocks[:, 2:7:4, :]}
         u_pairs = keep.tile([P, 2, W, 2], BF16, name="u_pairs")
         u_words = {h: keep.tile([P, W, PACK], BF16, name="u_words%d" % h, align_bytes=64) for h in late}
         q_words = keep.tile([P, NQ, PACK], BF16, name="q_words", align_bytes=64)
@@ -82,14 +80,9 @@ def tile_attend_pre_transe_f_topk_kernel(tc, qT, kT, rT, qn, offs, offs2, out):
         def slots(h):
             return slice(h * W, (h + 1) * W)
 
-        def add_early(h):
-            by_twos = "p t (g i) -> p g t i"
+        def pack_early(h):
             dst = u_words[h][:, :, 0:2] if h in late else u_pairs[:, 0, :, :]
-            add(
-                dst.rearrange("p (g i) t -> p g t i", i=2),
-                k_got[:, 0:2, slots(h)].rearrange(by_twos, i=2),
-                r_got[:, 0:2, slots(h)].rearrange(by_twos, i=2),
-            )
+            move("s", dst, u_early[:, :, slots(h)].rearrange("p t n -> p n t"))
 
         def pack(eng, h):
             move(eng, u_words[h][:, :, 2:4], late[h].rearrange("p t n -> p n t"))
@@ -103,10 +96,10 @@ def tile_attend_pre_transe_f_topk_kernel(tc, qT, kT, rT, qn, offs, offs2, out):
             move(eng, r_got[:, t, :], r_tab[:, t, :].indirect(r_list[:]))
 
         def gather_k(eng, t, lo, hi):
-            move(eng, k_got[:, t, lo:hi], k_tab[t].indirect(k_list[:, lo // 16 : hi // 16]))
+            move(eng, k_got[:, t, lo:hi], k_tab[t][:].indirect(k_list[:, lo // 16 : hi // 16]))
 
         def gather_last(eng, h):
-            move(eng, k_last[h][:], k_tab[3].indirect(k_list[:, 8 * h : 8 * h + 8]))
+            move(eng, k_last[h][:], k_tab[3][:].indirect(k_list[:, 8 * h : 8 * h + 8]))
 
         def add_late(t, h, k_cols):
             dst = late[h][:, t - 2, :] if h in late else u_pairs[:, 1, :, t - 2]
@@ -132,22 +125,25 @@ def tile_attend_pre_transe_f_topk_kernel(tc, qT, kT, rT, qn, offs, offs2, out):
             quantise(q_codes[c][:], q_scales[c][:], q_words[:, c * P : (c + 1) * P, :])
 
         for t in range(PACK):
-            gather_r("vvvs"[t], t)
+            gather_r("vvss"[t], t)
         gather_k("v", 0, 0, N)
-        gather_k("s", 1, 0, N)
+        add(u_early[:, 0, :], k_got[:, 0, :], r_got[:, 0, :])
+        gather_k("v", 1, 0, HALF)
+        gather_k("s", 1, HALF, N)
+        add(u_early[:, 1, :], k_got[:, 1, :], r_got[:, 1, :])
         for h in range(CH):
-            add_early(h)
-        gather_k("s", 2, 0, N)
-        for h in range(CH):
-            add_late(2, h, k_got[:, 2, slots(h)])
+            pack_early(h)
+        gather_k("v", 2, 0, N)
+        add(shared[:, : N - W], k_got[:, 2, W:], r_got[:, 2, W:])
+        add_late(2, 0, k_got[:, 2, :W])
 
-        for h in range(CH):
+        for h in (1, 0, 2, 3):
             gather_last("vvss"[h], h)
         cast_q("s", q_first, 0, 0, P // 2)
         cast_q("s", q_first, 0, P // 2, P)
-        add_last(0)
         add_last(1)
-        pack("v", 0)
+        add_last(0)
+        pack("v", 1)
         add_last(2)
         add_last(3)
         pack("s", 2)
@@ -155,10 +151,10 @@ def tile_attend_pre_transe_f_topk_kernel(tc, qT, kT, rT, qn, offs, offs2, out):
         pack("s", 3)
         nc.scalar.activation(out=bias[:], in_=qn_raw[:], func=COPY, scale=-0.5)
         quantise_q(0)
-        quantise_u(0, "k_last3")
-        weave(1, "k_last2")
+        quantise_u(1, "k_last3")
+        weave(0, "k_last2")
         cast_q("v", q_rest, P, P + S_CAST, NQ)
-        quantise_u(1, "u_codes1")
+        quantise_u(0, "u_codes0")
         quantise_q(1)
         quantise_u(2, "u_codes2")
         quantise_u(3, "u_codes3")
@@ -191,6 +187,6 @@ def tile_attend_pre_transe_f_topk_kernel(tc, qT, kT, rT, qn, offs, offs2, out):
 
         for a in range(2):
             for c in range(QT):
-                for h in (2 * a, 2 * a + 1):
+                for h in ((1, 0), (2, 3))[a]:
                     leave(res[a][:, c, slots(h % 2)], product(h, c)[:], c, "v" if a == 1 else "s")
                 store(a, c)

from contextlib import ExitStack

import concourse.mybir as mybir

N, T, R, D, NQ = 512, 2048, 1024, 512, 256
FLOPS = 2 * D * NQ * N

F32 = mybir.dt.float32
BF16 = mybir.dt.bfloat16
U32 = mybir.dt.uint32
U16 = mybir.dt.uint16
U8 = mybir.dt.uint8
FP8X4 = mybir.dt.float8_e4m3fn_x4
ADD = mybir.AluOpType.add
COPY = mybir.ActivationFunctionType.Copy
IDENTITY = mybir.ActivationFunctionType.Identity

P = 128
PACK = 4
HALF = N // 2
QT = NQ // P
W = 128
CH = N // W
S_CAST = 96
I32 = mybir.dt.int32


def tile_attend_pre_transe_f_topk_kernel(tc, qT, kT, rT, qn, offs, offs2, out):
    nc = tc.nc
    with ExitStack() as ctx:
        keep = ctx.enter_context(tc.tile_pool(name="keep", bufs=1))
        psum = ctx.enter_context(tc.psum_pool(name="psum", bufs=1))

        k_list = keep.tile([P, N // 16], U16, name="k_list")
        r_list = keep.tile([P, N // 16], U16, name="r_list")
        k_rows = kT.rearrange("(p t) n -> p t n", t=PACK)
        r_rows = rT.rearrange("(p t) n -> p t n", t=PACK)
        q_rows = qT[0].rearrange("(p t) q -> p t q", t=PACK)
        k_tab = [keep.tile([P, T], F32, name="k_tab%d" % t) for t in range(PACK)]
        r_tab = keep.tile([P, PACK, R], F32, name="r_tab")
        shared = keep.tile([P, N + 2 * PACK * P], BF16, name="shared", align_bytes=64)
        q_first = shared[:, N:].bitcast(F32).rearrange("p (t q) -> p t q", t=PACK)
        blocks = shared[:].rearrange("p (b n) -> p b n", n=W)
        q_rest = keep.tile([P, PACK, P], F32, name="q_rest", align_bytes=64)
        qn_raw = keep.tile([P, QT], F32, name="qn_raw")

        nc.sync.dma_start(out=r_tab[:], in_=r_rows)
        nc.sync.dma_start(r_list[:], offs2)
        nc.sync.dma_start(k_list[:], offs)
        for t in range(PACK):
            nc.sync.dma_start(out=k_tab[t][:], in_=k_rows[:, t, :])
        nc.sync.dma_start(out=q_first, in_=q_rows[:, :, :P])
        nc.sync.dma_start(out=q_rest[:], in_=q_rows[:, :, P:])
        with nc.allow_non_contiguous_dma(reason="one squared length a partition and query tile"):
            nc.sync.dma_start(out=qn_raw[:], in_=qn[0].rearrange("(c p) o -> p (c o)", c=QT))

        k_got = keep.tile([P, PACK - 1, N], F32, name="k_got")
        r_got = keep.tile([P, PACK, N], F32, name="r_got")
        k_last = [keep.tile([P, W], F32, name="k_last%d" % h, align_bytes=64) for h in range(CH)]
        u_early = keep.tile([P, 2, N], BF16, name="u_early")
        late = {1: blocks[:, 0:4:3, :], 2: blocks[:, 1:5:3, :], 3: blocks[:, 2:7:4, :]}
        u_pairs = keep.tile([P, 2, W, 2], BF16, name="u_pairs")
        u_words = {h: keep.tile([P, W, PACK], BF16, name="u_words%d" % h, align_bytes=64) for h in late}
        q_words = keep.tile([P, NQ, PACK], BF16, name="q_words", align_bytes=64)
        u_codes = {}
        u_scales = [keep.tile([P, W], U8, name="u_scales%d" % h, align_bytes=64) for h in range(CH)]
        q_codes = [keep.tile([P, P], U32, name="q_codes%d" % c, align_bytes=64) for c in range(QT)]
        q_scales = [keep.tile([P, P], U8, name="q_scales%d" % c, align_bytes=64) for c in range(QT)]
        bias = keep.tile([P, QT], F32, name="bias")

        def move(eng, dst, src):
            if eng == "v":
                nc.vector.tensor_copy(out=dst, in_=src)
            else:
                nc.scalar.activation(out=dst, in_=src, func=COPY)

        def add(dst, k_cols, r_cols):
            nc.vector.tensor_tensor(out=dst, in0=k_cols, in1=r_cols, op=ADD)

        def slots(h):
            return slice(h * W, (h + 1) * W)

        def pack_early(h):
            dst = u_words[h][:, :, 0:2] if h in late else u_pairs[:, 0, :, :]
            move("s", dst, u_early[:, :, slots(h)].rearrange("p t n -> p n t"))

        def pack(eng, h):
            move(eng, u_words[h][:, :, 2:4], late[h].rearrange("p t n -> p n t"))

        def cast_q(eng, raw, first, lo, hi):
            dst = q_words[:, lo:hi, :].rearrange("p (g i) t -> p g t i", i=2)
            src = raw[:, :, lo - first : hi - first].rearrange("p t (g i) -> p g t i", i=2)
            move(eng, dst, src)

        def gather_r(eng, t):
            move(eng, r_got[:, t, :], r_tab[:, t, :].indirect(r_list[:]))

        def gather_k(eng, t, lo, hi):
            move(eng, k_got[:, t, lo:hi], k_tab[t][:].indirect(k_list[:, lo // 16 : hi // 16]))

        def gather_last(eng, h):
            move(eng, k_last[h][:], k_tab[3][:].indirect(k_list[:, 8 * h : 8 * h + 8]))

        def add_late(t, h, k_cols):
            dst = late[h][:, t - 2, :] if h in late else u_pairs[:, 1, :, t - 2]
            add(dst, k_cols, r_got[:, t, slots(h)])

        def add_last(h):
            add_late(3, h, k_last[h][:])

        def weave(h, slot):
            u_words.setdefault(h, keep.tile([P, W, PACK], BF16, name="u_words%d" % h, tag=slot, align_bytes=64))
            src = u_pairs[:].rearrange("p j n e -> p j (n e)").bitcast(I32)
            dst = u_words[h][:].rearrange("p n t -> p (n t)").bitcast(I32)
            nc.vector.tensor_copy(out=dst.rearrange("p (n j) -> p n j", j=2), in_=src.rearrange("p j n -> p n j"))

        def quantise(codes, scales, words):
            nc.vector.quantize_mx(out=codes.bitcast(FP8X4), scales=scales, in_=words.rearrange("p m t -> p (m t)"))

        def quantise_u(h, slot):
            u_codes.setdefault(h, keep.tile([P, W], U32, name="u_codes%d" % h, tag=slot, align_bytes=64))
            quantise(u_codes[h][:], u_scales[h][:], u_words[h][:])

        def quantise_q(c):
            quantise(q_codes[c][:], q_scales[c][:], q_words[:, c * P : (c + 1) * P, :])

        for t in range(PACK):
            gather_r("vvss"[t], t)
        gather_k("v", 0, 0, N)
        add(u_early[:, 0, :], k_got[:, 0, :], r_got[:, 0, :])
        gather_k("v", 1, 0, HALF)
        gather_k("s", 1, HALF, N)
        add(u_early[:, 1, :], k_got[:, 1, :], r_got[:, 1, :])
        for h in range(CH):
            pack_early(h)
        gather_k("v", 2, 0, N)
        add(shared[:, : N - W], k_got[:, 2, W:], r_got[:, 2, W:])
        add_late(2, 0, k_got[:, 2, :W])

        for h in (1, 0, 2, 3):
            gather_last("vvss"[h], h)
        cast_q("s", q_first, 0, 0, P // 2)
        cast_q("s", q_first, 0, P // 2, P)
        add_last(1)
        add_last(0)
        pack("v", 1)
        add_last(2)
        add_last(3)
        pack("s", 2)
        cast_q("s", q_rest, P, P, P + S_CAST)
        pack("s", 3)
        nc.scalar.activation(out=bias[:], in_=qn_raw[:], func=COPY, scale=-0.5)
        quantise_q(0)
        quantise_u(1, "k_last3")
        weave(0, "k_last2")
        cast_q("v", q_rest, P, P + S_CAST, NQ)
        quantise_u(0, "u_codes0")
        quantise_q(1)
        quantise_u(2, "u_codes2")
        quantise_u(3, "u_codes3")

        res = [keep.tile([P, QT, HALF], F32, name="res%d" % a) for a in range(2)]
        out_rows = out[0].rearrange("(c p) n -> p c n", c=QT)

        def product(h, c):
            acc = psum.tile([P, W], F32, name="acc%d%d" % (h, c))
            nc.tensor.matmul_mx(
                out=acc[:],
                lhsT=q_codes[c][:].bitcast(FP8X4),
                lhsT_scale=q_scales[c][:],
                rhs=u_codes[h][:].bitcast(FP8X4),
                rhs_scale=u_scales[h][:],
                start=True,
                stop=True,
            )
            return acc

        def leave(dst, acc, c, eng):
            if eng == "v":
                nc.vector.tensor_scalar(out=dst, in0=acc, scalar1=bias[:, c : c + 1], scalar2=None, op0=ADD)
            else:
                nc.scalar.activation(out=dst, in_=acc, func=IDENTITY, bias=bias[:, c : c + 1])

        def store(a, c):
            eng = nc.scalar if c == 1 else nc.sync
            eng.dma_start(out=out_rows[:, c, a * HALF : (a + 1) * HALF], in_=res[a][:, c, :])

        for a in range(2):
            for c in range(QT):
                for h in ((1, 0), (2, 3))[a]:
                    leave(res[a][:, c, slots(h % 2)], product(h, c)[:], c, "v" if a == 1 else "s")
                store(a, c)
